import numpy as np
import ml_dtypes


def mxq(x, axis, fmt="e4m3"):
    dtype, down = {"e4m3": (ml_dtypes.float8_e4m3fn, 7), "e5m2": (ml_dtypes.float8_e5m2, 14)}[fmt]
    v = np.moveaxis(np.asarray(x, np.float32).astype(ml_dtypes.bfloat16).astype(np.float64), axis, -1)
    blocks = v.reshape(v.shape[:-1] + (-1, 32))
    amax = np.abs(blocks).max(-1, keepdims=True)
    byte = np.maximum(np.where(amax > 0, np.frexp(amax)[1] - 1 + 127, 0) - down, 1)
    scale = np.exp2(byte - 127.0)
    codes = (blocks / scale).astype(np.float32).astype(dtype).astype(np.float64)
    return np.moveaxis((codes * scale).reshape(v.shape), -1, axis)


WIDE = False


def mx_kscale(k):
    if not WIDE:
        return np.ones(k)
    levels = np.array([10, -10, 5, -5, 0])
    if k % 512:
        return np.exp2(np.random.permutation(np.resize(levels, k // 32))).repeat(32)
    a = np.empty((k // 512, 16))
    for p in range(k // 512):
        a[p, :8] = np.random.permutation(np.resize(levels, 8))
        for g in range(8):
            far = levels[np.abs(levels - a[p, g]) >= 10]
            a[p, g + 8] = far[np.random.randint(len(far))]
    return np.exp2(a.ravel()).repeat(32)


BF16 = ml_dtypes.bfloat16


def bf(x):
    return np.asarray(x, np.float32).astype(BF16)


def f64(x):
    return np.asarray(x).astype(np.float64)


E2M1 = np.array([0.0, 0.5, 1.0, 1.5, 2.0, 3.0, 4.0, 6.0, -0.0, -0.5, -1.0, -1.5, -2.0, -3.0, -4.0, -6.0])


def pack_weight(w, fmt):
    k, n = w.shape
    w = f64(bf(w)).reshape(k // 32, 32, n)
    amax = np.abs(w).max(1)
    if fmt == "e4m3":
        byte = np.frexp(amax)[1] - 1 + 127 - 7
    else:
        mant, ex = np.frexp(amax / 6.0)
        byte = np.where(mant > 0.5, ex, ex - 1) + 127
    byte = np.clip(np.where(amax > 0, byte, 1), 1, 254)
    scaled = (w * np.exp2(127.0 - byte)[:, None, :]).reshape(k, n).astype(np.float32)
    by_word = np.ascontiguousarray(scaled.reshape(k // 512, 128, 4, n).transpose(0, 1, 3, 2))
    if fmt == "e4m3":
        words = by_word.astype(ml_dtypes.float8_e4m3fn).view(np.uint8)
    else:
        c = by_word.astype(ml_dtypes.float4_e2m1fn).view(np.uint8) & 0xF
        words = c[..., 0::2] | (c[..., 1::2] << 4)
    return np.ascontiguousarray(words), np.ascontiguousarray(byte.astype(np.uint8).reshape(k // 512, 16, n))


def unpack_weight(words, scales, fmt):
    g, p, n, _ = words.shape
    if fmt == "e4m3":
        vals = np.ascontiguousarray(words).view(ml_dtypes.float8_e4m3fn).astype(np.float64)
    else:
        nib = np.empty((g, p, n, 4), np.uint8)
        nib[..., 0::2] = words & 0xF
        nib[..., 1::2] = words >> 4
        vals = E2M1[nib]
    vals = vals * np.repeat(np.exp2(scales.astype(np.float64) - 127.0), 8, axis=1)[..., None]
    return vals.transpose(0, 1, 3, 2).reshape(g * 512, n)
def pack4(w):
    words, scales = pack_weight(w, "e2m1")
    return words.reshape(words.shape[0], 128, -1), scales


def unpack4(words, scales):
    return unpack_weight(words.reshape(words.shape[0], 128, -1, 2), scales, "e2m1")


A, B, K, T = 512, 1536, 2048, 1024


def setup_inputs():
    s = mx_kscale(K)
    t = mx_kscale(B)
    gmap = np.random.standard_normal((B, K)) / np.sqrt(K)
    base = np.random.standard_normal((K, T))
    offset = 0.3 * np.random.standard_normal(B)
    member = np.random.random_sample((B, A)) < 0.5
    w = member * np.random.standard_normal((B, A)) / np.sqrt(B / 2)
    w_words, w_scales = pack4(w / t[:, None])
    return {"gmap": bf(gmap * s * t[:, None]),
            "base": bf(base / s[:, None]),
            "offset": bf(offset * t),
            "w_words": w_words,
            "w_scales": w_scales}


def reference(gmap, base, offset, w_words, w_scales):
    bottom = mxq(f64(gmap), 1, "e4m3") @ mxq(f64(base), 0, "e4m3")
    clipped = np.maximum(bottom + f64(offset)[:, None], 0.0)
    w = unpack4(w_words, w_scales)
    return w.T @ mxq(clipped, 0, "e4m3")

@@ -1,0 +1,276 @@
+from contextlib import ExitStack
+
+import concourse.mybir as mybir
+from concourse.masks import make_identity
+
+A, B, K, T = 512, 1536, 2048, 1024
+FLOPS = 2 * B * K * T + 2 * A * B * T
+
+F32 = mybir.dt.float32
+BF16 = mybir.dt.bfloat16
+I32 = mybir.dt.int32
+U32 = mybir.dt.uint32
+U8 = mybir.dt.uint8
+FP8X4 = mybir.dt.float8_e4m3fn_x4
+FP4X4 = mybir.dt.float4_e2m1fn_x4
+ACT = mybir.ActivationFunctionType
+
+P = 128
+PACK = 4
+KP = P * PACK
+N = 512
+PASSES = K // KP
+GROUPS = B // KP
+HALVES = T // N
+RUN = 4
+HEAD_VECTOR_COLS = 384
+
+
+def tile_mint_forecast_reconciliation_s13_kernel(tc, gmap, base, offset, w_words, w_scales, out):
+    nc = tc.nc
+    with ExitStack() as ctx:
+        keep = ctx.enter_context(tc.tile_pool(name="keep", bufs=1))
+        work = ctx.enter_context(tc.tile_pool(name="work", bufs=2))
+        psum = ctx.enter_context(tc.psum_pool(name="psum", bufs=1))
+        ctx.enter_context(tc.manual_schedule())
+
+        ident = keep.tile([P, P], F32, name="ident")
+        make_identity(nc, ident[:])
+        w_codes = keep.tile([P, GROUPS, 2 * A], U8, name="w_codes", align_bytes=64)
+        w_plane = keep.tile([P, GROUPS, A], U8, name="w_plane", align_bytes=64)
+        nc.gpsimd.memset(w_plane[:].rearrange("p g a -> p (g a)").bitcast(I32), 0)
+
+        offset_bf16 = keep.tile([P, GROUPS, PACK], BF16, name="offset_bf16")
+        nc.scalar.dma_start(out=offset_bf16[:], in_=offset.rearrange("(g p t) -> p g t", p=P, t=PACK))
+        bias = keep.tile([P, GROUPS, PACK], F32, name="bias")
+        nc.scalar.activation(out=bias[:], in_=offset_bf16[:], func=ACT.Identity)
+
+        g_raw, g_sorted, g_banks, g_grouped, g_quant = {}, {}, {}, {}, {}
+        x_raw, x_grouped, x_quant = {}, {}, {}
+        acc, h_raw, h_grouped, h_quant = {}, {}, {}, {}
+        turn_banks, acc_banks = [], []
+
+        def turn_bank():
+            n = len(turn_banks)
+            bank = psum.tile([P, N], F32, name="turn%d" % (n % 4))
+            turn_banks.append(bank)
+            return bank
+
+        def acc_bank():
+            n = len(acc_banks)
+            bank = psum.tile([P, N], F32, name="acc%d" % (n % 4))
+            acc_banks.append(bank)
+            return bank
+
+        def load_g(i):
+            raw = keep.tile([P, PACK, KP], BF16, name="g_raw%d" % i, align_bytes=64)
+            g, j = divmod(i, PACK)
+            rows = gmap[g * KP:(g + 1) * KP, :].rearrange("(m t) k -> m t k", t=PACK)
+            if g == 0:
+                nc.sync.dma_start(out=raw[:], in_=rows[:, :, j * KP:(j + 1) * KP])
+            else:
+                nc.sync.dma_start(out=raw[:].rearrange("p c k -> p (c k)"), in_=rows[:, j, :])
+            g_raw[i] = raw
+
+        def load_x(c, h):
+            raw = keep.tile([P, PACK, N], BF16, name="x_raw%d_%d" % (c, h), align_bytes=64)
+            nc.sync.dma_start(
+                out=raw[:],
+                in_=base[c * KP:(c + 1) * KP, h * N:(h + 1) * N].rearrange("(p j) n -> p j n", j=PACK))
+            x_raw[(c, h)] = raw
+
+        def load_w():
+            nc.sync.dma_start(out=w_codes[:].bitcast(I32), in_=w_words.rearrange("g p n -> p g n").bitcast(I32))
+            for q in range(4):
+                nc.sync.dma_start(
+                    out=w_plane[32 * q:32 * q + 4, :, :].bitcast(I32),
+                    in_=w_scales[:, 4 * q:4 * q + 4, :].rearrange("g r a -> r g a").bitcast(I32))
+
+        def sort_g(i):
+            words = g_raw[i][:].rearrange("p j k -> p (j k)").bitcast(F32)
+            srt = work.tile([P, 2 * KP], F32, name="g_sorted", align_bytes=64)
+            nc.vector.tensor_copy(
+                out=srt[:].rearrange("p (u b i) -> p b u i", u=2, i=RUN),
+                in_=words.rearrange("p (b i u) -> p b u i", u=2, i=RUN))
+            g_sorted[i] = srt
+
+        def transpose_g(i):
+            banks = []
+            for half in range(2):
+                bank = turn_bank()
+                for jj in range(2):
+                    j = 2 * half + jj
+                    for u in range(2):
+                        if i in g_sorted:
+                            src = g_sorted[i][:, u * KP + j * P:u * KP + (j + 1) * P]
+                        else:
+                            words = g_raw[i][:].rearrange("p j k -> p (j k)").bitcast(F32)
+                            src = words[:, 2 * P * j + u:2 * P * (j + 1):2]
+                        col = (2 * jj + u) * P
+                        nc.tensor.transpose(bank[:, col:col + P], src, ident[:])
+                banks.append(bank)
+            g_banks[i] = banks
+
+        def evacuate_g(i):
+            grouped = work.tile([P, PACK * N], BF16, name="g_grouped", bufs=3, align_bytes=64)
+            words = grouped[:].bitcast(F32)
+            for half in range(2):
+                nc.scalar.copy(
+                    out=words[:, half * N:(half + 1) * N].rearrange("p (j r u) -> p j r u", j=2, u=2),
+                    in_=g_banks[i][half][:].rearrange("p (j u r) -> p j r u", j=2, u=2))
+            g_grouped[i] = grouped
+
+        def quantize(grouped, name):
+            codes = keep.tile([P, N], U32, name=name + "_codes", align_bytes=64)
+            plane = keep.tile([P, N], U8, name=name + "_plane", align_bytes=64)
+            nc.vector.quantize_mx(out=codes[:].bitcast(FP8X4), scales=plane[:], in_=grouped[:])
+            return codes, plane
+
+        def quantize_g(i):
+            g_quant[i] = quantize(g_grouped[i], "g%d" % i)
+
+        def interleave(copy, grouped, raw, lo, hi):
+            copy(out=grouped[:, PACK * lo:PACK * hi].rearrange("p (c i t) -> p c t i", i=RUN, t=PACK),
+                 in_=raw[:, :, lo:hi].rearrange("p t (c i) -> p c t i", i=RUN))
+
+        def interleave_x(c, h, vector_cols=N):
+            grouped = work.tile([P, PACK * N], BF16, name="x_grouped", align_bytes=64)
+            interleave(nc.vector.tensor_copy, grouped, x_raw[(c, h)], 0, vector_cols)
+            if vector_cols < N:
+                interleave(nc.scalar.copy, grouped, x_raw[(c, h)], vector_cols, N)
+            x_grouped[(c, h)] = grouped
+
+        def quantize_x(c, h):
+            x_quant[(c, h)] = quantize(x_grouped[(c, h)], "x%d_%d" % (c, h))
+
+        def first_pass(g, t, h, c):
+            if c == 0:
+                acc[(g, t, h)] = acc_bank()
+            piece, j = (c, t) if g == 0 else (PACK * g + t, c)
+            g_codes, g_plane = g_quant[piece]
+            x_codes, x_plane = x_quant[(c, h)]
+            nc.tensor.matmul_mx(
+                out=acc[(g, t, h)][:],
+                lhsT=g_codes[:, j * P:(j + 1) * P].bitcast(FP8X4), lhsT_scale=g_plane[:, j * P:(j + 1) * P],
+                rhs=x_codes[:].bitcast(FP8X4), rhs_scale=x_plane[:],
+                start=(c == 0), stop=(c == PASSES - 1))
+
+        def first_product(g, t, h):
+            for c in range(PASSES):
+                first_pass(g, t, h, c)
+
+        def head_pass(c):
+            for t in range(PACK):
+                first_pass(0, t, 0, c)
+
+        def clip(g, t, h):
+            if t == 0:
+                h_raw[(g, h)] = keep.tile([P, PACK, N], BF16, name="h_raw%d_%d" % (g, h), align_bytes=64)
+            nc.scalar.activation(out=h_raw[(g, h)][:, t, :], in_=acc[(g, t, h)][:], func=ACT.Relu,
+                                 bias=bias[:, g, t:t + 1])
+
+        def interleave_h(g, h):
+            grouped = work.tile([P, PACK * N], BF16, name="h_grouped", align_bytes=64)
+            interleave(nc.vector.tensor_copy, grouped, h_raw[(g, h)], 0, N)
+            h_grouped[(g, h)] = grouped
+
+        def quantize_h(g, h):
+            h_quant[(g, h)] = quantize(h_grouped[(g, h)], "h%d_%d" % (g, h))
+
+        def second_product(a, h):
+            bank = turn_bank()
+            for g in range(GROUPS):
+                h_codes, h_plane = h_quant[(g, h)]
+                nc.tensor.matmul_mx(
+                    out=bank[:],
+                    lhsT=w_codes[:, g, 2 * a * P:2 * (a + 1) * P].bitcast(FP4X4),
+                    lhsT_scale=w_plane[:, g, a * P:(a + 1) * P],
+                    rhs=h_codes[:].bitcast(FP8X4), rhs_scale=h_plane[:],
+                    start=(g == 0), stop=(g == GROUPS - 1))
+            result = work.tile([P, N], F32, name="result", bufs=4)
+            copy = nc.scalar.copy if a % 2 == 0 else nc.vector.tensor_copy
+            copy(out=result[:], in_=bank[:])
+            nc.sync.dma_start(out=out[a * P:(a + 1) * P, h * N:(h + 1) * N], in_=result[:])
+
+        for c in range(PASSES):
+            load_g(c)
+            load_x(c, 0)
+        for pair in range(2):
+            load_g(4 + 2 * pair)
+            load_g(5 + 2 * pair)
+            load_x(2 * pair, 1)
+            load_x(2 * pair + 1, 1)
+        for i in range(8, 12):
+            load_g(i)
+        load_w()
+
+        for c in range(PASSES):
+            transpose_g(c)
+            if c > 0:
+                head_pass(c - 1)
+            evacuate_g(c)
+            interleave_x(c, 0, HEAD_VECTOR_COLS)
+            quantize_g(c)
+            quantize_x(c, 0)
+
+        transpose_g(4)
+        evacuate_g(4)
+        transpose_g(5)
+        evacuate_g(5)
+        head_pass(3)
+        interleave_x(0, 1)
+        quantize_g(4)
+        quantize_x(0, 1)
+        quantize_g(5)
+        for t in range(PACK):
+            clip(0, t, 0)
+        first_product(1, 0, 0)
+        interleave_x(1, 1)
+        interleave_x(2, 1)
+        quantize_x(1, 1)
+        transpose_g(6)
+        evacuate_g(6)
+        transpose_g(7)
+        clip(1, 0, 0)
+        evacuate_g(7)
+        quantize_g(6)
+        quantize_x(2, 1)
+        quantize_g(7)
+        for t in range(1, PACK):
+            first_product(1, t, 0)
+            clip(1, t, 0)
+        sort_g(8)
+        sort_g(9)
+        interleave_x(3, 1)
+        interleave_h(0, 0)
+        quantize_x(3, 1)
+        quantize_h(0, 0)
+
+        for g in range(2):
+            for i in (8 + 2 * g, 9 + 2 * g):
+                transpose_g(i)
+                evacuate_g(i)
+            if g == 0:
+                sort_g(10)
+                sort_g(11)
+            quantize_g(8 + 2 * g)
+            interleave_h(1 - g, g)
+            quantize_g(9 + 2 * g)
+            quantize_h(1 - g, g)
+            for t in range(PACK):
+                first_product(g, t, 1)
+                clip(g, t, 1)
+
+        previous = (1, 1)
+        for h in range(HALVES):
+            interleave_h(*previous)
+            quantize_h(*previous)
+            for t in range(PACK):
+                first_product(2, t, h)
+                clip(2, t, h)
+            previous = (2, h)
+        interleave_h(*previous)
+        quantize_h(*previous)
+        for h in range(HALVES):
+            for a in range(A // P):
+                second_product(a, h)

@@ -24,6 +24,7 @@ GROUPS = B // KP
 HALVES = T // N
 RUN = 4
 HEAD_VECTOR_COLS = 384
+WARM_FIRST, WARM_SECOND, WARM_THIRD = 8, 11, 3
 
 
 def tile_mint_forecast_reconciliation_s13_kernel(tc, gmap, base, offset, w_words, w_scales, out):
@@ -36,9 +37,8 @@ def tile_mint_forecast_reconciliation_s13_kernel(tc, gmap, base, offset, w_words
 
         ident = keep.tile([P, P], F32, name="ident")
         make_identity(nc, ident[:])
-        w_codes = keep.tile([P, GROUPS, 2 * A], U8, name="w_codes", align_bytes=64)
-        w_plane = keep.tile([P, GROUPS, A], U8, name="w_plane", align_bytes=64)
-        nc.gpsimd.memset(w_plane[:].rearrange("p g a -> p (g a)").bitcast(I32), 0)
+        w_codes = keep.tile([P, GROUPS, 2 * A], U8, name="w_codes", align_bytes=256)
+        w_plane = keep.tile([P, GROUPS, A], U8, name="w_plane", align_bytes=256)
 
         offset_bf16 = keep.tile([P, GROUPS, PACK], BF16, name="offset_bf16")
         nc.scalar.dma_start(out=offset_bf16[:], in_=offset.rearrange("(g p t) -> p g t", p=P, t=PACK))
@@ -49,6 +49,7 @@ def tile_mint_forecast_reconciliation_s13_kernel(tc, gmap, base, offset, w_words
         x_raw, x_grouped, x_quant = {}, {}, {}
         acc, h_raw, h_grouped, h_quant = {}, {}, {}, {}
         turn_banks, acc_banks = [], []
+        g_words = {}
 
         def turn_bank():
             n = len(turn_banks)
@@ -62,18 +63,37 @@ def tile_mint_forecast_reconciliation_s13_kernel(tc, gmap, base, offset, w_words
             acc_banks.append(bank)
             return bank
 
-        def load_g(i):
-            raw = keep.tile([P, PACK, KP], BF16, name="g_raw%d" % i, align_bytes=64)
+        ones = keep.tile([P, KP], BF16, name="ones", align_bytes=256)
+        warm_codes = keep.tile([P, P], U32, name="warm_codes", align_bytes=256)
+        warm_plane = keep.tile([P, P], U8, name="warm_plane", align_bytes=256)
+        nc.vector.memset(ones[:], 1.0)
+        nc.vector.quantize_mx(out=warm_codes[:].bitcast(FP8X4), scales=warm_plane[:], in_=ones[:])
+        nc.vector.memset(w_plane[:].rearrange("p g a -> p (g a)").bitcast(I32), 0)
+
+        def warm_up(passes):
+            bank = psum.tile([P, N], F32, name="acc3")
+            for n in range(passes):
+                nc.tensor.matmul_mx(
+                    out=bank[:, (n % 4) * P:(n % 4 + 1) * P],
+                    lhsT=warm_codes[:].bitcast(FP8X4), lhsT_scale=warm_plane[:],
+                    rhs=warm_codes[:].bitcast(FP8X4), rhs_scale=warm_plane[:], start=True, stop=True)
+
+        def load_g(i, half=None):
             g, j = divmod(i, PACK)
             rows = gmap[g * KP:(g + 1) * KP, :].rearrange("(m t) k -> m t k", t=PACK)
+            first, n = (0, PACK) if half is None else (2 * half, 2)
+            raw = keep.tile([P, n, KP], BF16, name="g_raw%d_%d" % (i, first), align_bytes=256)
             if g == 0:
-                nc.sync.dma_start(out=raw[:], in_=rows[:, :, j * KP:(j + 1) * KP])
+                nc.sync.dma_start(out=raw[:], in_=rows[:, first:first + n, j * KP:(j + 1) * KP])
             else:
                 nc.sync.dma_start(out=raw[:].rearrange("p c k -> p (c k)"), in_=rows[:, j, :])
+            words = raw[:].rearrange("p j k -> p (j k)").bitcast(F32)
+            for jj in range(n):
+                g_words[(i, first + jj)] = words[:, 2 * P * jj:2 * P * (jj + 1)]
             g_raw[i] = raw
 
         def load_x(c, h):
-            raw = keep.tile([P, PACK, N], BF16, name="x_raw%d_%d" % (c, h), align_bytes=64)
+            raw = keep.tile([P, PACK, N], BF16, name="x_raw%d_%d" % (c, h), align_bytes=256)
             nc.sync.dma_start(
                 out=raw[:],
                 in_=base[c * KP:(c + 1) * KP, h * N:(h + 1) * N].rearrange("(p j) n -> p j n", j=PACK))
@@ -88,15 +108,14 @@ def tile_mint_forecast_reconciliation_s13_kernel(tc, gmap, base, offset, w_words
 
         def sort_g(i):
             words = g_raw[i][:].rearrange("p j k -> p (j k)").bitcast(F32)
-            srt = work.tile([P, 2 * KP], F32, name="g_sorted", align_bytes=64)
+            srt = work.tile([P, 2 * KP], F32, name="g_sorted", align_bytes=256)
             nc.vector.tensor_copy(
                 out=srt[:].rearrange("p (u b i) -> p b u i", u=2, i=RUN),
                 in_=words.rearrange("p (b i u) -> p b u i", u=2, i=RUN))
             g_sorted[i] = srt
 
-        def transpose_g(i):
-            banks = []
-            for half in range(2):
+        def transpose_g(i, halves=(0, 1)):
+            for half in halves:
                 bank = turn_bank()
                 for jj in range(2):
                     j = 2 * half + jj
@@ -104,41 +123,49 @@ def tile_mint_forecast_reconciliation_s13_kernel(tc, gmap, base, offset, w_words
                         if i in g_sorted:
                             src = g_sorted[i][:, u * KP + j * P:u * KP + (j + 1) * P]
                         else:
-                            words = g_raw[i][:].rearrange("p j k -> p (j k)").bitcast(F32)
-                            src = words[:, 2 * P * j + u:2 * P * (j + 1):2]
+                            src = g_words[(i, j)][:, u:2 * P:2]
                         col = (2 * jj + u) * P
                         nc.tensor.transpose(bank[:, col:col + P], src, ident[:])
-                banks.append(bank)
-            g_banks[i] = banks
+                g_banks[(i, half)] = bank
 
-        def evacuate_g(i):
-            grouped = work.tile([P, PACK * N], BF16, name="g_grouped", bufs=3, align_bytes=64)
-            words = grouped[:].bitcast(F32)
-            for half in range(2):
+        def evacuate_g(i, halves=(0, 1)):
+            if halves[0] == 0:
+                g_grouped[i] = work.tile([P, PACK * N], BF16, name="g_grouped", bufs=3, align_bytes=256)
+            words = g_grouped[i][:].bitcast(F32)
+            for half in halves:
                 nc.scalar.copy(
                     out=words[:, half * N:(half + 1) * N].rearrange("p (j r u) -> p j r u", j=2, u=2),
-                    in_=g_banks[i][half][:].rearrange("p (j u r) -> p j r u", j=2, u=2))
-            g_grouped[i] = grouped
+                    in_=g_banks[(i, half)][:].rearrange("p (j u r) -> p j r u", j=2, u=2))
+
+        def mx_tiles(name):
+            codes = keep.tile([P, N], U32, name=name + "_codes", align_bytes=256)
+            plane = keep.tile([P, N], U8, name=name + "_plane", align_bytes=256)
+            return codes, plane
 
         def quantize(grouped, name):
-            codes = keep.tile([P, N], U32, name=name + "_codes", align_bytes=64)
-            plane = keep.tile([P, N], U8, name=name + "_plane", align_bytes=64)
+            codes, plane = mx_tiles(name)
             nc.vector.quantize_mx(out=codes[:].bitcast(FP8X4), scales=plane[:], in_=grouped[:])
             return codes, plane
 
         def quantize_g(i):
             g_quant[i] = quantize(g_grouped[i], "g%d" % i)
 
+        def quantize_g_half(i, half):
+            if half == 0:
+                g_quant[i] = mx_tiles("g%d" % i)
+            codes, plane = g_quant[i]
+            cols = slice(half * N // 2, (half + 1) * N // 2)
+            nc.vector.quantize_mx(out=codes[:, cols].bitcast(FP8X4), scales=plane[:, cols],
+                                  in_=g_grouped[i][:, half * 2 * N:(half + 1) * 2 * N])
+
         def interleave(copy, grouped, raw, lo, hi):
             copy(out=grouped[:, PACK * lo:PACK * hi].rearrange("p (c i t) -> p c t i", i=RUN, t=PACK),
                  in_=raw[:, :, lo:hi].rearrange("p t (c i) -> p c t i", i=RUN))
 
-        def interleave_x(c, h, vector_cols=N):
-            grouped = work.tile([P, PACK * N], BF16, name="x_grouped", align_bytes=64)
-            interleave(nc.vector.tensor_copy, grouped, x_raw[(c, h)], 0, vector_cols)
-            if vector_cols < N:
-                interleave(nc.scalar.copy, grouped, x_raw[(c, h)], vector_cols, N)
-            x_grouped[(c, h)] = grouped
+        def interleave_x(c, h, lo=0, hi=N, copy=nc.vector.tensor_copy):
+            if (c, h) not in x_grouped:
+                x_grouped[(c, h)] = work.tile([P, PACK * N], BF16, name="x_grouped", align_bytes=256)
+            interleave(copy, x_grouped[(c, h)], x_raw[(c, h)], lo, hi)
 
         def quantize_x(c, h):
             x_quant[(c, h)] = quantize(x_grouped[(c, h)], "x%d_%d" % (c, h))
@@ -165,19 +192,19 @@ def tile_mint_forecast_reconciliation_s13_kernel(tc, gmap, base, offset, w_words
 
         def clip(g, t, h):
             if t == 0:
-                h_raw[(g, h)] = keep.tile([P, PACK, N], BF16, name="h_raw%d_%d" % (g, h), align_bytes=64)
+                h_raw[(g, h)] = work.tile([P, PACK, N], BF16, name="h_raw", bufs=4, align_bytes=256)
             nc.scalar.activation(out=h_raw[(g, h)][:, t, :], in_=acc[(g, t, h)][:], func=ACT.Relu,
                                  bias=bias[:, g, t:t + 1])
 
         def interleave_h(g, h):
-            grouped = work.tile([P, PACK * N], BF16, name="h_grouped", align_bytes=64)
+            grouped = work.tile([P, PACK * N], BF16, name="h_grouped", align_bytes=256)
             interleave(nc.vector.tensor_copy, grouped, h_raw[(g, h)], 0, N)
             h_grouped[(g, h)] = grouped
 
         def quantize_h(g, h):
             h_quant[(g, h)] = quantize(h_grouped[(g, h)], "h%d_%d" % (g, h))
 
-        def second_product(a, h):
+        def second_product(a, h, parts=1):
             bank = turn_bank()
             for g in range(GROUPS):
                 h_codes, h_plane = h_quant[(g, h)]
@@ -187,12 +214,20 @@ def tile_mint_forecast_reconciliation_s13_kernel(tc, gmap, base, offset, w_words
                     lhsT_scale=w_plane[:, g, a * P:(a + 1) * P],
                     rhs=h_codes[:].bitcast(FP8X4), rhs_scale=h_plane[:],
                     start=(g == 0), stop=(g == GROUPS - 1))
-            result = work.tile([P, N], F32, name="result", bufs=4)
-            copy = nc.scalar.copy if a % 2 == 0 else nc.vector.tensor_copy
-            copy(out=result[:], in_=bank[:])
-            nc.sync.dma_start(out=out[a * P:(a + 1) * P, h * N:(h + 1) * N], in_=result[:])
+            width = N // parts
+            for part in range(parts):
+                result = work.tile([P, width], F32, name="result", bufs=6)
+                nc.scalar.copy(out=result[:], in_=bank[:, part * width:(part + 1) * width])
+                first = h * N + part * width
+                nc.sync.dma_start(out=out[a * P:(a + 1) * P, first:first + width], in_=result[:])
 
-        for c in range(PASSES):
+        load_g(0, 0)
+        load_x(0, 0)
+        load_g(0, 1)
+        load_g(1, 0)
+        load_g(1, 1)
+        load_x(1, 0)
+        for c in range(2, PASSES):
             load_g(c)
             load_x(c, 0)
         for pair in range(2):
@@ -204,47 +239,73 @@ def tile_mint_forecast_reconciliation_s13_kernel(tc, gmap, base, offset, w_words
             load_g(i)
         load_w()
 
-        for c in range(PASSES):
+        warm_up(WARM_FIRST)
+        transpose_g(0, (0,))
+        warm_up(WARM_SECOND)
+        transpose_g(0, (1,))
+        evacuate_g(0, (0,))
+        interleave_x(0, 0, 0, HEAD_VECTOR_COLS)
+        interleave_x(0, 0, HEAD_VECTOR_COLS, N, nc.scalar.copy)
+        quantize_g_half(0, 0)
+        quantize_x(0, 0)
+        evacuate_g(0, (1,))
+        quantize_g_half(0, 1)
+        transpose_g(1, (0,))
+        evacuate_g(1, (0,))
+        warm_up(WARM_THIRD)
+        head_pass(0)
+        interleave_x(1, 0, 0, HEAD_VECTOR_COLS)
+        interleave_x(1, 0, HEAD_VECTOR_COLS, N, nc.scalar.copy)
+        quantize_g_half(1, 0)
+        quantize_x(1, 0)
+        transpose_g(1, (1,))
+        evacuate_g(1, (1,))
+        quantize_g_half(1, 1)
+        for c in range(2, PASSES):
             transpose_g(c)
-            if c > 0:
-                head_pass(c - 1)
+            head_pass(c - 1)
             evacuate_g(c)
-            interleave_x(c, 0, HEAD_VECTOR_COLS)
+            interleave_x(c, 0, 0, HEAD_VECTOR_COLS)
+            interleave_x(c, 0, HEAD_VECTOR_COLS, N, nc.scalar.copy)
             quantize_g(c)
             quantize_x(c, 0)
 
         transpose_g(4)
         evacuate_g(4)
         transpose_g(5)
-        evacuate_g(5)
+        evacuate_g(5, (0,))
         head_pass(3)
-        interleave_x(0, 1)
+        clip(0, 0, 0)
+        evacuate_g(5, (1,))
+        interleave_x(0, 1, 0, N // 2)
         quantize_g(4)
+        interleave_x(0, 1, N // 2, N)
+        interleave_x(1, 1)
         quantize_x(0, 1)
         quantize_g(5)
-        for t in range(PACK):
+        quantize_x(1, 1)
+        for t in range(1, PACK):
             clip(0, t, 0)
         first_product(1, 0, 0)
-        interleave_x(1, 1)
-        interleave_x(2, 1)
-        quantize_x(1, 1)
         transpose_g(6)
         evacuate_g(6)
         transpose_g(7)
-        clip(1, 0, 0)
         evacuate_g(7)
+        interleave_x(2, 1, 0, N // 2)
         quantize_g(6)
-        quantize_x(2, 1)
+        interleave_x(2, 1, N // 2, N)
         quantize_g(7)
+        quantize_x(2, 1)
+        clip(1, 0, 0)
         for t in range(1, PACK):
             first_product(1, t, 0)
+            if t == 3:
+                interleave_x(3, 1, N // 2, N, nc.scalar.copy)
             clip(1, t, 0)
         sort_g(8)
         sort_g(9)
-        interleave_x(3, 1)
-        interleave_h(0, 0)
+        interleave_x(3, 1, 0, N // 2)
         quantize_x(3, 1)
-        quantize_h(0, 0)
 
         for g in range(2):
             for i in (8 + 2 * g, 9 + 2 * g):
@@ -253,24 +314,24 @@ def tile_mint_forecast_reconciliation_s13_kernel(tc, gmap, base, offset, w_words
             if g == 0:
                 sort_g(10)
                 sort_g(11)
+            interleave_h(g, 0)
             quantize_g(8 + 2 * g)
-            interleave_h(1 - g, g)
+            quantize_h(g, 0)
             quantize_g(9 + 2 * g)
-            quantize_h(1 - g, g)
             for t in range(PACK):
                 first_product(g, t, 1)
                 clip(g, t, 1)
 
-        previous = (1, 1)
+        interleave_h(0, 1)
+        interleave_h(1, 1)
+        quantize_h(0, 1)
+        quantize_h(1, 1)
         for h in range(HALVES):
-            interleave_h(*previous)
-            quantize_h(*previous)
             for t in range(PACK):
                 first_product(2, t, h)
                 clip(2, t, h)
-            previous = (2, h)
-        interleave_h(*previous)
-        quantize_h(*previous)
+            interleave_h(2, h)
+            quantize_h(2, h)
         for h in range(HALVES):
             for a in range(A // P):
-                second_product(a, h)
+                second_product(a, h, 2 if (h, a) == (1, 3) else 1)

@@ -24,7 +24,8 @@ GROUPS = B // KP
 HALVES = T // N
 RUN = 4
 HEAD_VECTOR_COLS = 384
-WARM_FIRST, WARM_SECOND, WARM_THIRD = 8, 11, 3
+LATE_VECTOR_COLS = 256
+WARM_FIRST, WARM_SECOND, WARM_THIRD = 8, 9, 4
 
 
 def tile_mint_forecast_reconciliation_s13_kernel(tc, gmap, base, offset, w_words, w_scales, out):
@@ -40,10 +41,7 @@ def tile_mint_forecast_reconciliation_s13_kernel(tc, gmap, base, offset, w_words
         w_codes = keep.tile([P, GROUPS, 2 * A], U8, name="w_codes", align_bytes=256)
         w_plane = keep.tile([P, GROUPS, A], U8, name="w_plane", align_bytes=256)
 
-        offset_bf16 = keep.tile([P, GROUPS, PACK], BF16, name="offset_bf16")
-        nc.scalar.dma_start(out=offset_bf16[:], in_=offset.rearrange("(g p t) -> p g t", p=P, t=PACK))
-        bias = keep.tile([P, GROUPS, PACK], F32, name="bias")
-        nc.scalar.activation(out=bias[:], in_=offset_bf16[:], func=ACT.Identity)
+        bias = keep.tile([P, GROUPS, PACK], BF16, name="bias")
 
         g_raw, g_sorted, g_banks, g_grouped, g_quant = {}, {}, {}, {}, {}
         x_raw, x_grouped, x_quant = {}, {}, {}
@@ -106,6 +104,12 @@ def tile_mint_forecast_reconciliation_s13_kernel(tc, gmap, base, offset, w_words
                     out=w_plane[32 * q:32 * q + 4, :, :].bitcast(I32),
                     in_=w_scales[:, 4 * q:4 * q + 4, :].rearrange("g r a -> r g a").bitcast(I32))
 
+        def load_offset():
+            nc.sync.dma_start(out=bias[:], in_=offset.rearrange("(g p t) -> p g t", p=P, t=PACK))
+
+        def scalar_copy_values(out, in_):
+            nc.scalar.activation(out=out, in_=in_, func=ACT.Copy)
+
         def sort_g(i):
             words = g_raw[i][:].rearrange("p j k -> p (j k)").bitcast(F32)
             srt = work.tile([P, 2 * KP], F32, name="g_sorted", align_bytes=256)
@@ -164,7 +168,7 @@ def tile_mint_forecast_reconciliation_s13_kernel(tc, gmap, base, offset, w_words
 
         def interleave_x(c, h, lo=0, hi=N, copy=nc.vector.tensor_copy):
             if (c, h) not in x_grouped:
-                x_grouped[(c, h)] = work.tile([P, PACK * N], BF16, name="x_grouped", align_bytes=256)
+                x_grouped[(c, h)] = work.tile([P, PACK * N], BF16, name="x_grouped", bufs=3, align_bytes=256)
             interleave(copy, x_grouped[(c, h)], x_raw[(c, h)], lo, hi)
 
         def quantize_x(c, h):
@@ -186,15 +190,19 @@ def tile_mint_forecast_reconciliation_s13_kernel(tc, gmap, base, offset, w_words
             for c in range(PASSES):
                 first_pass(g, t, h, c)
 
-        def head_pass(c):
+        def head_pass(c, h=0):
             for t in range(PACK):
-                first_pass(0, t, 0, c)
+                first_pass(0, t, h, c)
 
-        def clip(g, t, h):
+        def clip(g, t, h, on_vector=False):
             if t == 0:
                 h_raw[(g, h)] = work.tile([P, PACK, N], BF16, name="h_raw", bufs=4, align_bytes=256)
-            nc.scalar.activation(out=h_raw[(g, h)][:, t, :], in_=acc[(g, t, h)][:], func=ACT.Relu,
-                                 bias=bias[:, g, t:t + 1])
+            if on_vector:
+                nc.vector.tensor_scalar(out=h_raw[(g, h)][:, t, :], in0=acc[(g, t, h)][:], scalar1=bias[:, g, t:t + 1],
+                                        scalar2=0.0, op0=mybir.AluOpType.add, op1=mybir.AluOpType.max)
+            else:
+                nc.scalar.activation(out=h_raw[(g, h)][:, t, :], in_=acc[(g, t, h)][:], func=ACT.Relu,
+                                     bias=bias[:, g, t:t + 1])
 
         def interleave_h(g, h):
             grouped = work.tile([P, PACK * N], BF16, name="h_grouped", align_bytes=256)
@@ -227,14 +235,18 @@ def tile_mint_forecast_reconciliation_s13_kernel(tc, gmap, base, offset, w_words
         load_g(1, 0)
         load_g(1, 1)
         load_x(1, 0)
-        for c in range(2, PASSES):
-            load_g(c)
-            load_x(c, 0)
-        for pair in range(2):
-            load_g(4 + 2 * pair)
-            load_g(5 + 2 * pair)
-            load_x(2 * pair, 1)
-            load_x(2 * pair + 1, 1)
+        load_g(2)
+        load_x(2, 0)
+        load_g(3)
+        load_g(4)
+        load_x(3, 0)
+        load_g(5)
+        load_offset()
+        load_x(0, 1)
+        load_g(6)
+        load_g(7)
+        for c in range(1, PASSES):
+            load_x(c, 1)
         for i in range(8, 12):
             load_g(i)
         load_w()
@@ -243,11 +255,11 @@ def tile_mint_forecast_reconciliation_s13_kernel(tc, gmap, base, offset, w_words
         transpose_g(0, (0,))
         warm_up(WARM_SECOND)
         transpose_g(0, (1,))
-        evacuate_g(0, (0,))
         interleave_x(0, 0, 0, HEAD_VECTOR_COLS)
-        interleave_x(0, 0, HEAD_VECTOR_COLS, N, nc.scalar.copy)
-        quantize_g_half(0, 0)
+        interleave_x(0, 0, HEAD_VECTOR_COLS, N, scalar_copy_values)
+        evacuate_g(0, (0,))
         quantize_x(0, 0)
+        quantize_g_half(0, 0)
         evacuate_g(0, (1,))
         quantize_g_half(0, 1)
         transpose_g(1, (0,))
@@ -265,6 +277,8 @@ def tile_mint_forecast_reconciliation_s13_kernel(tc, gmap, base, offset, w_words
             transpose_g(c)
             head_pass(c - 1)
             evacuate_g(c)
+            if c == 3:
+                sort_g(4)
             interleave_x(c, 0, 0, HEAD_VECTOR_COLS)
             interleave_x(c, 0, HEAD_VECTOR_COLS, N, nc.scalar.copy)
             quantize_g(c)
@@ -277,50 +291,63 @@ def tile_mint_forecast_reconciliation_s13_kernel(tc, gmap, base, offset, w_words
         head_pass(3)
         clip(0, 0, 0)
         evacuate_g(5, (1,))
-        interleave_x(0, 1, 0, N // 2)
         quantize_g(4)
-        interleave_x(0, 1, N // 2, N)
-        interleave_x(1, 1)
-        quantize_x(0, 1)
+        interleave_x(0, 1)
+        sort_g(6)
         quantize_g(5)
-        quantize_x(1, 1)
-        for t in range(1, PACK):
-            clip(0, t, 0)
+        sort_g(7)
+        quantize_x(0, 1)
+        clip(0, 1, 0)
+        clip(0, 2, 0)
         first_product(1, 0, 0)
         transpose_g(6)
         evacuate_g(6)
         transpose_g(7)
         evacuate_g(7)
-        interleave_x(2, 1, 0, N // 2)
+        clip(0, 3, 0)
+        interleave_x(1, 1, 0, N // 2)
         quantize_g(6)
-        interleave_x(2, 1, N // 2, N)
+        interleave_x(1, 1, N // 2, N)
         quantize_g(7)
-        quantize_x(2, 1)
+        quantize_x(1, 1)
         clip(1, 0, 0)
         for t in range(1, PACK):
             first_product(1, t, 0)
-            if t == 3:
-                interleave_x(3, 1, N // 2, N, nc.scalar.copy)
             clip(1, t, 0)
+        interleave_x(2, 1)
+        interleave_x(3, 1, 0, LATE_VECTOR_COLS)
+        interleave_x(3, 1, LATE_VECTOR_COLS, N, nc.scalar.copy)
+        quantize_x(2, 1)
         sort_g(8)
-        sort_g(9)
-        interleave_x(3, 1, 0, N // 2)
         quantize_x(3, 1)
-
-        for g in range(2):
-            for i in (8 + 2 * g, 9 + 2 * g):
-                transpose_g(i)
-                evacuate_g(i)
-            if g == 0:
-                sort_g(10)
-                sort_g(11)
-            interleave_h(g, 0)
-            quantize_g(8 + 2 * g)
-            quantize_h(g, 0)
-            quantize_g(9 + 2 * g)
-            for t in range(PACK):
-                first_product(g, t, 1)
-                clip(g, t, 1)
+        for c in range(PASSES + 1):
+            for t in range(PACK - 1):
+                if c < PASSES:
+                    first_pass(0, t, 1, c)
+            if c > 0:
+                first_pass(0, PACK - 1, 1, c - 1)
+        sort_g(9)
+        for t in range(PACK):
+            clip(0, t, 1)
+        for i in (8, 9):
+            transpose_g(i)
+            evacuate_g(i)
+        sort_g(10)
+        sort_g(11)
+        interleave_h(0, 0)
+        quantize_g(8)
+        quantize_h(0, 0)
+        quantize_g(9)
+        interleave_h(1, 0)
+        for t in range(PACK):
+            first_product(1, t, 1)
+            clip(1, t, 1)
+        for i in (10, 11):
+            transpose_g(i)
+            evacuate_g(i)
+        quantize_h(1, 0)
+        quantize_g(10)
+        quantize_g(11)
 
         interleave_h(0, 1)
         interleave_h(1, 1)

@@ -17,15 +17,21 @@ ACT = mybir.ActivationFunctionType
 
 P = 128
 PACK = 4
-KP = P * PACK
+K_PASS = P * PACK
 N = 512
-PASSES = K // KP
-GROUPS = B // KP
+PASSES = K // K_PASS
+GROUPS = B // K_PASS
 HALVES = T // N
+PIECES = GROUPS * PACK
 RUN = 4
-HEAD_VECTOR_COLS = 384
-LATE_VECTOR_COLS = 256
-WARM_FIRST, WARM_SECOND, WARM_THIRD = 8, 9, 4
+ALIGN = 256
+QUADRANT = 32
+BANKS = 8
+HEAD_PIECES = 6
+
+FIRST_HALF_VECTOR_COLS = 384
+SECOND_HALF_VECTOR_COLS = 256
+WARM_FIRST, WARM_SECOND, WARM_THIRD = 8, 8, 3
 
 
 def tile_mint_forecast_reconciliation_s13_kernel(tc, gmap, base, offset, w_words, w_scales, out):
@@ -38,112 +44,101 @@ def tile_mint_forecast_reconciliation_s13_kernel(tc, gmap, base, offset, w_words
 
         ident = keep.tile([P, P], F32, name="ident")
         make_identity(nc, ident[:])
-        w_codes = keep.tile([P, GROUPS, 2 * A], U8, name="w_codes", align_bytes=256)
-        w_plane = keep.tile([P, GROUPS, A], U8, name="w_plane", align_bytes=256)
-
+        w_codes = keep.tile([P, GROUPS, 2 * A], U8, name="w_codes", align_bytes=ALIGN)
+        w_plane = keep.tile([P, GROUPS, A], U8, name="w_plane", align_bytes=ALIGN)
         bias = keep.tile([P, GROUPS, PACK], BF16, name="bias")
 
-        g_raw, g_sorted, g_banks, g_grouped, g_quant = {}, {}, {}, {}, {}
-        x_raw, x_grouped, x_quant = {}, {}, {}
-        acc, h_raw, h_grouped, h_quant = {}, {}, {}, {}
-        turn_banks, acc_banks = [], []
-        g_words = {}
-
-        def turn_bank():
-            n = len(turn_banks)
-            bank = psum.tile([P, N], F32, name="turn%d" % (n % 4))
-            turn_banks.append(bank)
-            return bank
-
-        def acc_bank():
-            n = len(acc_banks)
-            bank = psum.tile([P, N], F32, name="acc%d" % (n % 4))
-            acc_banks.append(bank)
-            return bank
-
-        ones = keep.tile([P, KP], BF16, name="ones", align_bytes=256)
-        warm_codes = keep.tile([P, P], U32, name="warm_codes", align_bytes=256)
-        warm_plane = keep.tile([P, P], U8, name="warm_plane", align_bytes=256)
+        ones = keep.tile([P, K_PASS], BF16, name="ones", align_bytes=ALIGN)
+        warm_codes = keep.tile([P, P], U32, name="warm_codes", align_bytes=ALIGN)
+        warm_plane = keep.tile([P, P], U8, name="warm_plane", align_bytes=ALIGN)
         nc.vector.memset(ones[:], 1.0)
         nc.vector.quantize_mx(out=warm_codes[:].bitcast(FP8X4), scales=warm_plane[:], in_=ones[:])
         nc.vector.memset(w_plane[:].rearrange("p g a -> p (g a)").bitcast(I32), 0)
 
+        g_words, g_raw, g_sorted, g_banks, g_grouped, g_quant = {}, {}, {}, {}, {}, {}
+        x_raw, x_grouped, x_quant = {}, {}, {}
+        sums, h_raw, h_grouped, h_quant = {}, {}, {}, {}
+        head_banks, ring_banks = [], []
+
+        def bank_tile(number):
+            bank = psum.tile([P, N], F32, name="bank%d" % number)
+            return bank
+
+        def ring_bank():
+            ring_banks.append(bank_tile((BANKS // 2 + len(ring_banks)) % BANKS))
+            return ring_banks[-1]
+
+        def head_bank():
+            head_banks.append(bank_tile(len(head_banks) % (BANKS // 2)))
+            return head_banks[-1]
+
         def warm_up(passes):
-            bank = psum.tile([P, N], F32, name="acc3")
+            bank = bank_tile(BANKS - 1)
             for n in range(passes):
+                first = n % (N // P) * P
                 nc.tensor.matmul_mx(
-                    out=bank[:, (n % 4) * P:(n % 4 + 1) * P],
+                    out=bank[:, first:first + P],
                     lhsT=warm_codes[:].bitcast(FP8X4), lhsT_scale=warm_plane[:],
                     rhs=warm_codes[:].bitcast(FP8X4), rhs_scale=warm_plane[:], start=True, stop=True)
 
-        def load_g(i, half=None):
-            g, j = divmod(i, PACK)
-            rows = gmap[g * KP:(g + 1) * KP, :].rearrange("(m t) k -> m t k", t=PACK)
-            first, n = (0, PACK) if half is None else (2 * half, 2)
-            raw = keep.tile([P, n, KP], BF16, name="g_raw%d_%d" % (i, first), align_bytes=256)
+        def load_g(piece, first=0, quarters=PACK):
+            g, j = divmod(piece, PACK)
+            rows = gmap[g * K_PASS:(g + 1) * K_PASS, :].rearrange("(m t) k -> m t k", t=PACK)
+            raw = keep.tile([P, quarters, K_PASS], BF16, name="g_raw%d_%d" % (piece, first), align_bytes=ALIGN)
             if g == 0:
-                nc.sync.dma_start(out=raw[:], in_=rows[:, first:first + n, j * KP:(j + 1) * KP])
+                nc.sync.dma_start(out=raw[:], in_=rows[:, first:first + quarters, j * K_PASS:(j + 1) * K_PASS])
             else:
                 nc.sync.dma_start(out=raw[:].rearrange("p c k -> p (c k)"), in_=rows[:, j, :])
-            words = raw[:].rearrange("p j k -> p (j k)").bitcast(F32)
-            for jj in range(n):
-                g_words[(i, first + jj)] = words[:, 2 * P * jj:2 * P * (jj + 1)]
-            g_raw[i] = raw
+            g_raw[piece] = raw[:].rearrange("p j k -> p (j k)").bitcast(F32)
+            for n in range(quarters):
+                g_words[(piece, first + n)] = g_raw[piece][:, 2 * P * n:2 * P * (n + 1)]
 
         def load_x(c, h):
-            raw = keep.tile([P, PACK, N], BF16, name="x_raw%d_%d" % (c, h), align_bytes=256)
-            nc.sync.dma_start(
-                out=raw[:],
-                in_=base[c * KP:(c + 1) * KP, h * N:(h + 1) * N].rearrange("(p j) n -> p j n", j=PACK))
+            raw = keep.tile([P, PACK, N], BF16, name="x_raw%d_%d" % (c, h), align_bytes=ALIGN)
+            rows = base[c * K_PASS:(c + 1) * K_PASS, h * N:(h + 1) * N]
+            nc.sync.dma_start(out=raw[:], in_=rows.rearrange("(p j) n -> p j n", j=PACK))
             x_raw[(c, h)] = raw
 
         def load_w():
             nc.sync.dma_start(out=w_codes[:].bitcast(I32), in_=w_words.rearrange("g p n -> p g n").bitcast(I32))
-            for q in range(4):
+            for q in range(P // QUADRANT):
                 nc.sync.dma_start(
-                    out=w_plane[32 * q:32 * q + 4, :, :].bitcast(I32),
+                    out=w_plane[QUADRANT * q:QUADRANT * q + 4, :, :].bitcast(I32),
                     in_=w_scales[:, 4 * q:4 * q + 4, :].rearrange("g r a -> r g a").bitcast(I32))
 
-        def load_offset():
-            nc.sync.dma_start(out=bias[:], in_=offset.rearrange("(g p t) -> p g t", p=P, t=PACK))
-
-        def scalar_copy_values(out, in_):
-            nc.scalar.activation(out=out, in_=in_, func=ACT.Copy)
-
-        def sort_g(i):
-            words = g_raw[i][:].rearrange("p j k -> p (j k)").bitcast(F32)
-            srt = work.tile([P, 2 * KP], F32, name="g_sorted", align_bytes=256)
+        def sort_g(piece):
+            ordered = work.tile([P, 2 * K_PASS], F32, name="g_sorted", align_bytes=ALIGN)
             nc.vector.tensor_copy(
-                out=srt[:].rearrange("p (u b i) -> p b u i", u=2, i=RUN),
-                in_=words.rearrange("p (b i u) -> p b u i", u=2, i=RUN))
-            g_sorted[i] = srt
+                out=ordered[:].rearrange("p (u b i) -> p b u i", u=2, i=RUN),
+                in_=g_raw[piece].rearrange("p (b i u) -> p b u i", u=2, i=RUN))
+            g_sorted[piece] = ordered
 
-        def transpose_g(i, halves=(0, 1)):
-            for half in halves:
-                bank = turn_bank()
-                for jj in range(2):
-                    j = 2 * half + jj
+        def transpose_g(piece, pairs=(0, 1)):
+            for pair in pairs:
+                bank = head_bank() if piece < HEAD_PIECES else ring_bank()
+                for n in range(2):
+                    quarter = 2 * pair + n
                     for u in range(2):
-                        if i in g_sorted:
-                            src = g_sorted[i][:, u * KP + j * P:u * KP + (j + 1) * P]
+                        if piece in g_sorted:
+                            words = g_sorted[piece][:, u * K_PASS + quarter * P:u * K_PASS + (quarter + 1) * P]
                         else:
-                            src = g_words[(i, j)][:, u:2 * P:2]
-                        col = (2 * jj + u) * P
-                        nc.tensor.transpose(bank[:, col:col + P], src, ident[:])
-                g_banks[(i, half)] = bank
+                            words = g_words[(piece, quarter)][:, u:2 * P:2]
+                        first = (2 * n + u) * P
+                        nc.tensor.transpose(bank[:, first:first + P], words, ident[:])
+                g_banks[(piece, pair)] = bank
 
-        def evacuate_g(i, halves=(0, 1)):
-            if halves[0] == 0:
-                g_grouped[i] = work.tile([P, PACK * N], BF16, name="g_grouped", bufs=3, align_bytes=256)
-            words = g_grouped[i][:].bitcast(F32)
-            for half in halves:
+        def evacuate_g(piece, pairs=(0, 1)):
+            if pairs[0] == 0:
+                g_grouped[piece] = work.tile([P, PACK * N], BF16, name="g_grouped", bufs=3, align_bytes=ALIGN)
+            words = g_grouped[piece][:].bitcast(F32)
+            for pair in pairs:
                 nc.scalar.copy(
-                    out=words[:, half * N:(half + 1) * N].rearrange("p (j r u) -> p j r u", j=2, u=2),
-                    in_=g_banks[(i, half)][:].rearrange("p (j u r) -> p j r u", j=2, u=2))
+                    out=words[:, pair * N:(pair + 1) * N].rearrange("p (j r u) -> p j r u", j=2, u=2),
+                    in_=g_banks[(piece, pair)][:].rearrange("p (j u r) -> p j r u", j=2, u=2))
 
         def mx_tiles(name):
-            codes = keep.tile([P, N], U32, name=name + "_codes", align_bytes=256)
-            plane = keep.tile([P, N], U8, name=name + "_plane", align_bytes=256)
+            codes = keep.tile([P, N], U32, name=name + "_codes", align_bytes=ALIGN)
+            plane = keep.tile([P, N], U8, name=name + "_plane", align_bytes=ALIGN)
             return codes, plane
 
         def quantize(grouped, name):
@@ -151,16 +146,16 @@ def tile_mint_forecast_reconciliation_s13_kernel(tc, gmap, base, offset, w_words
             nc.vector.quantize_mx(out=codes[:].bitcast(FP8X4), scales=plane[:], in_=grouped[:])
             return codes, plane
 
-        def quantize_g(i):
-            g_quant[i] = quantize(g_grouped[i], "g%d" % i)
+        def quantize_g(piece):
+            g_quant[piece] = quantize(g_grouped[piece], "g%d" % piece)
 
-        def quantize_g_half(i, half):
-            if half == 0:
-                g_quant[i] = mx_tiles("g%d" % i)
-            codes, plane = g_quant[i]
-            cols = slice(half * N // 2, (half + 1) * N // 2)
+        def quantize_g_pair(piece, pair):
+            if pair == 0:
+                g_quant[piece] = mx_tiles("g%d" % piece)
+            codes, plane = g_quant[piece]
+            cols = slice(pair * 2 * P, (pair + 1) * 2 * P)
             nc.vector.quantize_mx(out=codes[:, cols].bitcast(FP8X4), scales=plane[:, cols],
-                                  in_=g_grouped[i][:, half * 2 * N:(half + 1) * 2 * N])
+                                  in_=g_grouped[piece][:, PACK * cols.start:PACK * cols.stop])
 
         def interleave(copy, grouped, raw, lo, hi):
             copy(out=grouped[:, PACK * lo:PACK * hi].rearrange("p (c i t) -> p c t i", i=RUN, t=PACK),
@@ -168,21 +163,29 @@ def tile_mint_forecast_reconciliation_s13_kernel(tc, gmap, base, offset, w_words
 
         def interleave_x(c, h, lo=0, hi=N, copy=nc.vector.tensor_copy):
             if (c, h) not in x_grouped:
-                x_grouped[(c, h)] = work.tile([P, PACK * N], BF16, name="x_grouped", bufs=3, align_bytes=256)
+                x_grouped[(c, h)] = work.tile([P, PACK * N], BF16, name="x_grouped", bufs=3, align_bytes=ALIGN)
             interleave(copy, x_grouped[(c, h)], x_raw[(c, h)], lo, hi)
+
+        def share_interleave_x(c, scalar_copy=nc.scalar.copy):
+            interleave_x(c, 0, 0, FIRST_HALF_VECTOR_COLS)
+            interleave_x(c, 0, FIRST_HALF_VECTOR_COLS, N, scalar_copy)
+
+        def copy_by_activation(out, in_):
+            nc.scalar.activation(out=out, in_=in_, func=ACT.Copy)
 
         def quantize_x(c, h):
             x_quant[(c, h)] = quantize(x_grouped[(c, h)], "x%d_%d" % (c, h))
 
         def first_pass(g, t, h, c):
             if c == 0:
-                acc[(g, t, h)] = acc_bank()
-            piece, j = (c, t) if g == 0 else (PACK * g + t, c)
+                sums[(g, t, h)] = ring_bank()
+            piece, quarter = (c, t) if g == 0 else (PACK * g + t, c)
             g_codes, g_plane = g_quant[piece]
             x_codes, x_plane = x_quant[(c, h)]
+            cols = slice(quarter * P, (quarter + 1) * P)
             nc.tensor.matmul_mx(
-                out=acc[(g, t, h)][:],
-                lhsT=g_codes[:, j * P:(j + 1) * P].bitcast(FP8X4), lhsT_scale=g_plane[:, j * P:(j + 1) * P],
+                out=sums[(g, t, h)][:],
+                lhsT=g_codes[:, cols].bitcast(FP8X4), lhsT_scale=g_plane[:, cols],
                 rhs=x_codes[:].bitcast(FP8X4), rhs_scale=x_plane[:],
                 start=(c == 0), stop=(c == PASSES - 1))
 
@@ -190,30 +193,26 @@ def tile_mint_forecast_reconciliation_s13_kernel(tc, gmap, base, offset, w_words
             for c in range(PASSES):
                 first_pass(g, t, h, c)
 
-        def head_pass(c, h=0):
+        def group0_pass(c, h):
             for t in range(PACK):
                 first_pass(0, t, h, c)
 
-        def clip(g, t, h, on_vector=False):
+        def clip(g, t, h):
             if t == 0:
-                h_raw[(g, h)] = work.tile([P, PACK, N], BF16, name="h_raw", bufs=4, align_bytes=256)
-            if on_vector:
-                nc.vector.tensor_scalar(out=h_raw[(g, h)][:, t, :], in0=acc[(g, t, h)][:], scalar1=bias[:, g, t:t + 1],
-                                        scalar2=0.0, op0=mybir.AluOpType.add, op1=mybir.AluOpType.max)
-            else:
-                nc.scalar.activation(out=h_raw[(g, h)][:, t, :], in_=acc[(g, t, h)][:], func=ACT.Relu,
-                                     bias=bias[:, g, t:t + 1])
+                h_raw[(g, h)] = work.tile([P, PACK, N], BF16, name="h_raw", bufs=4, align_bytes=ALIGN)
+            nc.scalar.activation(out=h_raw[(g, h)][:, t, :], in_=sums[(g, t, h)][:], func=ACT.Relu,
+                                 bias=bias[:, g, t:t + 1])
 
         def interleave_h(g, h):
-            grouped = work.tile([P, PACK * N], BF16, name="h_grouped", align_bytes=256)
+            grouped = work.tile([P, PACK * N], BF16, name="h_grouped", align_bytes=ALIGN)
             interleave(nc.vector.tensor_copy, grouped, h_raw[(g, h)], 0, N)
             h_grouped[(g, h)] = grouped
 
         def quantize_h(g, h):
             h_quant[(g, h)] = quantize(h_grouped[(g, h)], "h%d_%d" % (g, h))
 
-        def second_product(a, h, parts=1):
-            bank = turn_bank()
+        def second_product(a, h, stores):
+            bank = ring_bank()
             for g in range(GROUPS):
                 h_codes, h_plane = h_quant[(g, h)]
                 nc.tensor.matmul_mx(
@@ -222,18 +221,18 @@ def tile_mint_forecast_reconciliation_s13_kernel(tc, gmap, base, offset, w_words
                     lhsT_scale=w_plane[:, g, a * P:(a + 1) * P],
                     rhs=h_codes[:].bitcast(FP8X4), rhs_scale=h_plane[:],
                     start=(g == 0), stop=(g == GROUPS - 1))
-            width = N // parts
-            for part in range(parts):
+            width = N // stores
+            for part in range(stores):
                 result = work.tile([P, width], F32, name="result", bufs=6)
                 nc.scalar.copy(out=result[:], in_=bank[:, part * width:(part + 1) * width])
                 first = h * N + part * width
                 nc.sync.dma_start(out=out[a * P:(a + 1) * P, first:first + width], in_=result[:])
 
-        load_g(0, 0)
+        load_g(0, 0, 2)
         load_x(0, 0)
-        load_g(0, 1)
-        load_g(1, 0)
-        load_g(1, 1)
+        load_g(0, 2, 2)
+        load_g(1, 0, 2)
+        load_g(1, 2, 2)
         load_x(1, 0)
         load_g(2)
         load_x(2, 0)
@@ -241,99 +240,90 @@ def tile_mint_forecast_reconciliation_s13_kernel(tc, gmap, base, offset, w_words
         load_g(4)
         load_x(3, 0)
         load_g(5)
-        load_offset()
+        nc.sync.dma_start(out=bias[:], in_=offset.rearrange("(g p t) -> p g t", p=P, t=PACK))
         load_x(0, 1)
         load_g(6)
         load_g(7)
         for c in range(1, PASSES):
             load_x(c, 1)
-        for i in range(8, 12):
-            load_g(i)
+        for piece in range(2 * PACK, PIECES):
+            load_g(piece)
         load_w()
 
         warm_up(WARM_FIRST)
         transpose_g(0, (0,))
         warm_up(WARM_SECOND)
         transpose_g(0, (1,))
-        interleave_x(0, 0, 0, HEAD_VECTOR_COLS)
-        interleave_x(0, 0, HEAD_VECTOR_COLS, N, scalar_copy_values)
+        share_interleave_x(0, copy_by_activation)
         evacuate_g(0, (0,))
         quantize_x(0, 0)
-        quantize_g_half(0, 0)
+        quantize_g_pair(0, 0)
         evacuate_g(0, (1,))
-        quantize_g_half(0, 1)
+        quantize_g_pair(0, 1)
         transpose_g(1, (0,))
         evacuate_g(1, (0,))
         warm_up(WARM_THIRD)
-        head_pass(0)
-        interleave_x(1, 0, 0, HEAD_VECTOR_COLS)
-        interleave_x(1, 0, HEAD_VECTOR_COLS, N, nc.scalar.copy)
-        quantize_g_half(1, 0)
+        group0_pass(0, 0)
+        share_interleave_x(1)
+        quantize_g_pair(1, 0)
         quantize_x(1, 0)
         transpose_g(1, (1,))
         evacuate_g(1, (1,))
-        quantize_g_half(1, 1)
+        quantize_g_pair(1, 1)
         for c in range(2, PASSES):
             transpose_g(c)
-            head_pass(c - 1)
+            group0_pass(c - 1, 0)
             evacuate_g(c)
-            if c == 3:
+            if c == PASSES - 1:
                 sort_g(4)
-            interleave_x(c, 0, 0, HEAD_VECTOR_COLS)
-            interleave_x(c, 0, HEAD_VECTOR_COLS, N, nc.scalar.copy)
+            share_interleave_x(c)
             quantize_g(c)
             quantize_x(c, 0)
 
-        transpose_g(4)
-        evacuate_g(4)
-        transpose_g(5)
-        evacuate_g(5, (0,))
-        head_pass(3)
-        clip(0, 0, 0)
-        evacuate_g(5, (1,))
+        for piece in (4, 5):
+            transpose_g(piece)
+            evacuate_g(piece)
+        group0_pass(PASSES - 1, 0)
+        for t in range(PACK - 1):
+            clip(0, t, 0)
         quantize_g(4)
-        interleave_x(0, 1)
+        interleave_x(0, 1, 0, N // 2)
         sort_g(6)
-        quantize_g(5)
+        interleave_x(0, 1, N // 2, N)
         sort_g(7)
+        quantize_g(5)
         quantize_x(0, 1)
-        clip(0, 1, 0)
-        clip(0, 2, 0)
         first_product(1, 0, 0)
-        transpose_g(6)
-        evacuate_g(6)
-        transpose_g(7)
-        evacuate_g(7)
-        clip(0, 3, 0)
-        interleave_x(1, 1, 0, N // 2)
-        quantize_g(6)
-        interleave_x(1, 1, N // 2, N)
-        quantize_g(7)
-        quantize_x(1, 1)
+        for piece in (6, 7):
+            transpose_g(piece)
+            evacuate_g(piece)
+        clip(0, PACK - 1, 0)
         clip(1, 0, 0)
+        for c in (2, 3):
+            interleave_x(c, 1, SECOND_HALF_VECTOR_COLS, N, nc.scalar.copy)
+        quantize_g(6)
+        interleave_x(1, 1, 0, N // 2)
+        quantize_g(7)
+        interleave_x(1, 1, N // 2, N)
         for t in range(1, PACK):
             first_product(1, t, 0)
             clip(1, t, 0)
-        interleave_x(2, 1)
-        interleave_x(3, 1, 0, LATE_VECTOR_COLS)
-        interleave_x(3, 1, LATE_VECTOR_COLS, N, nc.scalar.copy)
-        quantize_x(2, 1)
-        sort_g(8)
-        quantize_x(3, 1)
-        for c in range(PASSES + 1):
-            for t in range(PACK - 1):
-                if c < PASSES:
-                    first_pass(0, t, 1, c)
-            if c > 0:
-                first_pass(0, PACK - 1, 1, c - 1)
-        sort_g(9)
+        for c in (2, 3):
+            interleave_x(c, 1, 0, SECOND_HALF_VECTOR_COLS)
+            quantize_x(c - 1, 1)
+        quantize_x(PASSES - 1, 1)
+
+        for c in range(PASSES):
+            group0_pass(c, 1)
+        for piece in (8, 9):
+            sort_g(piece)
         for t in range(PACK):
             clip(0, t, 1)
-        for i in (8, 9):
-            transpose_g(i)
-            evacuate_g(i)
-        sort_g(10)
-        sort_g(11)
+        for piece in (8, 9):
+            transpose_g(piece)
+            evacuate_g(piece)
+        for piece in (10, 11):
+            sort_g(piece)
         interleave_h(0, 0)
         quantize_g(8)
         quantize_h(0, 0)
@@ -342,23 +332,24 @@ def tile_mint_forecast_reconciliation_s13_kernel(tc, gmap, base, offset, w_words
         for t in range(PACK):
             first_product(1, t, 1)
             clip(1, t, 1)
-        for i in (10, 11):
-            transpose_g(i)
-            evacuate_g(i)
+        for piece in (10, 11):
+            transpose_g(piece)
+            evacuate_g(piece)
         quantize_h(1, 0)
-        quantize_g(10)
-        quantize_g(11)
+        for piece in (10, 11):
+            quantize_g(piece)
 
-        interleave_h(0, 1)
-        interleave_h(1, 1)
-        quantize_h(0, 1)
-        quantize_h(1, 1)
+        for g in range(2):
+            interleave_h(g, 1)
+        for g in range(2):
+            quantize_h(g, 1)
         for h in range(HALVES):
             for t in range(PACK):
                 first_product(2, t, h)
                 clip(2, t, h)
             interleave_h(2, h)
             quantize_h(2, h)
-        for h in range(HALVES):
-            for a in range(A // P):
-                second_product(a, h, 2 if (h, a) == (1, 3) else 1)
+
+        tiles = [(h, a) for h in range(HALVES) for a in range(A // P)]
+        for h, a in tiles:
+            second_product(a, h, 2 if (h, a) == tiles[-1] else 1)

@@ -26,12 +26,12 @@ PIECES = GROUPS * PACK
 RUN = 4
 ALIGN = 256
 QUADRANT = 32
+SCALE_ROWS = 4
 BANKS = 8
 HEAD_PIECES = 6
 
 FIRST_HALF_VECTOR_COLS = 384
 SECOND_HALF_VECTOR_COLS = 256
-WARM_FIRST, WARM_SECOND, WARM_THIRD = 8, 8, 3
 
 
 def tile_mint_forecast_reconciliation_s13_kernel(tc, gmap, base, offset, w_words, w_scales, out):
@@ -48,16 +48,11 @@ def tile_mint_forecast_reconciliation_s13_kernel(tc, gmap, base, offset, w_words
         w_plane = keep.tile([P, GROUPS, A], U8, name="w_plane", align_bytes=ALIGN)
         bias = keep.tile([P, GROUPS, PACK], BF16, name="bias")
 
-        ones = keep.tile([P, K_PASS], BF16, name="ones", align_bytes=ALIGN)
-        warm_codes = keep.tile([P, P], U32, name="warm_codes", align_bytes=ALIGN)
-        warm_plane = keep.tile([P, P], U8, name="warm_plane", align_bytes=ALIGN)
-        nc.vector.memset(ones[:], 1.0)
-        nc.vector.quantize_mx(out=warm_codes[:].bitcast(FP8X4), scales=warm_plane[:], in_=ones[:])
         nc.vector.memset(w_plane[:].rearrange("p g a -> p (g a)").bitcast(I32), 0)
 
-        g_words, g_raw, g_sorted, g_banks, g_grouped, g_quant = {}, {}, {}, {}, {}, {}
-        x_raw, x_grouped, x_quant = {}, {}, {}
-        sums, h_raw, h_grouped, h_quant = {}, {}, {}, {}
+        gmap_words, gmap_raw, gmap_sorted, gmap_banks, gmap_grouped, gmap_quant = {}, {}, {}, {}, {}, {}
+        base_raw, base_grouped, base_quant = {}, {}, {}
+        sums, clipped_raw, clipped_grouped, clipped_quant = {}, {}, {}, {}
         head_banks, ring_banks = [], []
 
         def bank_tile(number):
@@ -72,16 +67,7 @@ def tile_mint_forecast_reconciliation_s13_kernel(tc, gmap, base, offset, w_words
             head_banks.append(bank_tile(len(head_banks) % (BANKS // 2)))
             return head_banks[-1]
 
-        def warm_up(passes):
-            bank = bank_tile(BANKS - 1)
-            for n in range(passes):
-                first = n % (N // P) * P
-                nc.tensor.matmul_mx(
-                    out=bank[:, first:first + P],
-                    lhsT=warm_codes[:].bitcast(FP8X4), lhsT_scale=warm_plane[:],
-                    rhs=warm_codes[:].bitcast(FP8X4), rhs_scale=warm_plane[:], start=True, stop=True)
-
-        def load_g(piece, first=0, quarters=PACK):
+        def load_gmap(piece, first=0, quarters=PACK):
             g, j = divmod(piece, PACK)
             rows = gmap[g * K_PASS:(g + 1) * K_PASS, :].rearrange("(m t) k -> m t k", t=PACK)
             raw = keep.tile([P, quarters, K_PASS], BF16, name="g_raw%d_%d" % (piece, first), align_bytes=ALIGN)
@@ -89,52 +75,53 @@ def tile_mint_forecast_reconciliation_s13_kernel(tc, gmap, base, offset, w_words
                 nc.sync.dma_start(out=raw[:], in_=rows[:, first:first + quarters, j * K_PASS:(j + 1) * K_PASS])
             else:
                 nc.sync.dma_start(out=raw[:].rearrange("p c k -> p (c k)"), in_=rows[:, j, :])
-            g_raw[piece] = raw[:].rearrange("p j k -> p (j k)").bitcast(F32)
+            gmap_raw[piece] = raw[:].rearrange("p j k -> p (j k)").bitcast(F32)
             for n in range(quarters):
-                g_words[(piece, first + n)] = g_raw[piece][:, 2 * P * n:2 * P * (n + 1)]
+                gmap_words[(piece, first + n)] = gmap_raw[piece][:, 2 * P * n:2 * P * (n + 1)]
 
-        def load_x(c, h):
+        def load_base(c, h):
             raw = keep.tile([P, PACK, N], BF16, name="x_raw%d_%d" % (c, h), align_bytes=ALIGN)
             rows = base[c * K_PASS:(c + 1) * K_PASS, h * N:(h + 1) * N]
             nc.sync.dma_start(out=raw[:], in_=rows.rearrange("(p j) n -> p j n", j=PACK))
-            x_raw[(c, h)] = raw
+            base_raw[(c, h)] = raw
 
         def load_w():
             nc.sync.dma_start(out=w_codes[:].bitcast(I32), in_=w_words.rearrange("g p n -> p g n").bitcast(I32))
-            for q in range(P // QUADRANT):
+            for quadrant in range(P // QUADRANT):
+                rows = w_scales[:, SCALE_ROWS * quadrant:SCALE_ROWS * (quadrant + 1), :]
                 nc.sync.dma_start(
-                    out=w_plane[QUADRANT * q:QUADRANT * q + 4, :, :].bitcast(I32),
-                    in_=w_scales[:, 4 * q:4 * q + 4, :].rearrange("g r a -> r g a").bitcast(I32))
+                    out=w_plane[QUADRANT * quadrant:QUADRANT * quadrant + SCALE_ROWS, :, :].bitcast(I32),
+                    in_=rows.rearrange("g r a -> r g a").bitcast(I32))
 
-        def sort_g(piece):
+        def sort_gmap(piece):
             ordered = work.tile([P, 2 * K_PASS], F32, name="g_sorted", align_bytes=ALIGN)
             nc.vector.tensor_copy(
-                out=ordered[:].rearrange("p (u b i) -> p b u i", u=2, i=RUN),
-                in_=g_raw[piece].rearrange("p (b i u) -> p b u i", u=2, i=RUN))
-            g_sorted[piece] = ordered
+                out=ordered[:].rearrange("p (u run i) -> p run u i", u=2, i=RUN),
+                in_=gmap_raw[piece].rearrange("p (run i u) -> p run u i", u=2, i=RUN))
+            gmap_sorted[piece] = ordered
 
-        def transpose_g(piece, pairs=(0, 1)):
+        def transpose_gmap(piece, pairs=(0, 1)):
             for pair in pairs:
                 bank = head_bank() if piece < HEAD_PIECES else ring_bank()
                 for n in range(2):
                     quarter = 2 * pair + n
                     for u in range(2):
-                        if piece in g_sorted:
-                            words = g_sorted[piece][:, u * K_PASS + quarter * P:u * K_PASS + (quarter + 1) * P]
+                        if piece in gmap_sorted:
+                            words = gmap_sorted[piece][:, u * K_PASS + quarter * P:u * K_PASS + (quarter + 1) * P]
                         else:
-                            words = g_words[(piece, quarter)][:, u:2 * P:2]
-                        first = (2 * n + u) * P
-                        nc.tensor.transpose(bank[:, first:first + P], words, ident[:])
-                g_banks[(piece, pair)] = bank
+                            words = gmap_words[(piece, quarter)][:, u:2 * P:2]
+                        column = (2 * n + u) * P
+                        nc.tensor.transpose(bank[:, column:column + P], words, ident[:])
+                gmap_banks[(piece, pair)] = bank
 
-        def evacuate_g(piece, pairs=(0, 1)):
+        def evacuate_gmap(piece, pairs=(0, 1)):
             if pairs[0] == 0:
-                g_grouped[piece] = work.tile([P, PACK * N], BF16, name="g_grouped", bufs=3, align_bytes=ALIGN)
-            words = g_grouped[piece][:].bitcast(F32)
+                gmap_grouped[piece] = work.tile([P, PACK * N], BF16, name="g_grouped", bufs=3, align_bytes=ALIGN)
+            words = gmap_grouped[piece][:].bitcast(F32)
             for pair in pairs:
                 nc.scalar.copy(
                     out=words[:, pair * N:(pair + 1) * N].rearrange("p (j r u) -> p j r u", j=2, u=2),
-                    in_=g_banks[(piece, pair)][:].rearrange("p (j u r) -> p j r u", j=2, u=2))
+                    in_=gmap_banks[(piece, pair)][:].rearrange("p (j u r) -> p j r u", j=2, u=2))
 
         def mx_tiles(name):
             codes = keep.tile([P, N], U32, name=name + "_codes", align_bytes=ALIGN)
@@ -146,47 +133,47 @@ def tile_mint_forecast_reconciliation_s13_kernel(tc, gmap, base, offset, w_words
             nc.vector.quantize_mx(out=codes[:].bitcast(FP8X4), scales=plane[:], in_=grouped[:])
             return codes, plane
 
-        def quantize_g(piece):
-            g_quant[piece] = quantize(g_grouped[piece], "g%d" % piece)
+        def quantize_gmap(piece):
+            gmap_quant[piece] = quantize(gmap_grouped[piece], "g%d" % piece)
 
-        def quantize_g_pair(piece, pair):
+        def quantize_gmap_pair(piece, pair):
             if pair == 0:
-                g_quant[piece] = mx_tiles("g%d" % piece)
-            codes, plane = g_quant[piece]
+                gmap_quant[piece] = mx_tiles("g%d" % piece)
+            codes, plane = gmap_quant[piece]
             cols = slice(pair * 2 * P, (pair + 1) * 2 * P)
             nc.vector.quantize_mx(out=codes[:, cols].bitcast(FP8X4), scales=plane[:, cols],
-                                  in_=g_grouped[piece][:, PACK * cols.start:PACK * cols.stop])
+                                  in_=gmap_grouped[piece][:, PACK * cols.start:PACK * cols.stop])
 
         def interleave(copy, grouped, raw, lo, hi):
-            copy(out=grouped[:, PACK * lo:PACK * hi].rearrange("p (c i t) -> p c t i", i=RUN, t=PACK),
-                 in_=raw[:, :, lo:hi].rearrange("p t (c i) -> p c t i", i=RUN))
+            copy(out=grouped[:, PACK * lo:PACK * hi].rearrange("p (run i t) -> p run t i", i=RUN, t=PACK),
+                 in_=raw[:, :, lo:hi].rearrange("p t (run i) -> p run t i", i=RUN))
 
-        def interleave_x(c, h, lo=0, hi=N, copy=nc.vector.tensor_copy):
-            if (c, h) not in x_grouped:
-                x_grouped[(c, h)] = work.tile([P, PACK * N], BF16, name="x_grouped", bufs=3, align_bytes=ALIGN)
-            interleave(copy, x_grouped[(c, h)], x_raw[(c, h)], lo, hi)
+        def interleave_base(c, h, lo=0, hi=N, copy=nc.vector.tensor_copy):
+            if (c, h) not in base_grouped:
+                base_grouped[(c, h)] = work.tile([P, PACK * N], BF16, name="x_grouped", bufs=3, align_bytes=ALIGN)
+            interleave(copy, base_grouped[(c, h)], base_raw[(c, h)], lo, hi)
 
-        def share_interleave_x(c, scalar_copy=nc.scalar.copy):
-            interleave_x(c, 0, 0, FIRST_HALF_VECTOR_COLS)
-            interleave_x(c, 0, FIRST_HALF_VECTOR_COLS, N, scalar_copy)
+        def share_interleave_base(c, scalar_copy=nc.scalar.copy):
+            interleave_base(c, 0, 0, FIRST_HALF_VECTOR_COLS)
+            interleave_base(c, 0, FIRST_HALF_VECTOR_COLS, N, scalar_copy)
 
         def copy_by_activation(out, in_):
             nc.scalar.activation(out=out, in_=in_, func=ACT.Copy)
 
-        def quantize_x(c, h):
-            x_quant[(c, h)] = quantize(x_grouped[(c, h)], "x%d_%d" % (c, h))
+        def quantize_base(c, h):
+            base_quant[(c, h)] = quantize(base_grouped[(c, h)], "x%d_%d" % (c, h))
 
         def first_pass(g, t, h, c):
             if c == 0:
                 sums[(g, t, h)] = ring_bank()
             piece, quarter = (c, t) if g == 0 else (PACK * g + t, c)
-            g_codes, g_plane = g_quant[piece]
-            x_codes, x_plane = x_quant[(c, h)]
+            gmap_codes, gmap_plane = gmap_quant[piece]
+            base_codes, base_plane = base_quant[(c, h)]
             cols = slice(quarter * P, (quarter + 1) * P)
             nc.tensor.matmul_mx(
                 out=sums[(g, t, h)][:],
-                lhsT=g_codes[:, cols].bitcast(FP8X4), lhsT_scale=g_plane[:, cols],
-                rhs=x_codes[:].bitcast(FP8X4), rhs_scale=x_plane[:],
+                lhsT=gmap_codes[:, cols].bitcast(FP8X4), lhsT_scale=gmap_plane[:, cols],
+                rhs=base_codes[:].bitcast(FP8X4), rhs_scale=base_plane[:],
                 start=(c == 0), stop=(c == PASSES - 1))
 
         def first_product(g, t, h):
@@ -199,156 +186,152 @@ def tile_mint_forecast_reconciliation_s13_kernel(tc, gmap, base, offset, w_words
 
         def clip(g, t, h):
             if t == 0:
-                h_raw[(g, h)] = work.tile([P, PACK, N], BF16, name="h_raw", bufs=4, align_bytes=ALIGN)
-            nc.scalar.activation(out=h_raw[(g, h)][:, t, :], in_=sums[(g, t, h)][:], func=ACT.Relu,
+                clipped_raw[(g, h)] = work.tile([P, PACK, N], BF16, name="h_raw", bufs=4, align_bytes=ALIGN)
+            nc.scalar.activation(out=clipped_raw[(g, h)][:, t, :], in_=sums[(g, t, h)][:], func=ACT.Relu,
                                  bias=bias[:, g, t:t + 1])
 
-        def interleave_h(g, h):
+        def interleave_clipped(g, h):
             grouped = work.tile([P, PACK * N], BF16, name="h_grouped", align_bytes=ALIGN)
-            interleave(nc.vector.tensor_copy, grouped, h_raw[(g, h)], 0, N)
-            h_grouped[(g, h)] = grouped
+            interleave(nc.vector.tensor_copy, grouped, clipped_raw[(g, h)], 0, N)
+            clipped_grouped[(g, h)] = grouped
 
-        def quantize_h(g, h):
-            h_quant[(g, h)] = quantize(h_grouped[(g, h)], "h%d_%d" % (g, h))
+        def quantize_clipped(g, h):
+            clipped_quant[(g, h)] = quantize(clipped_grouped[(g, h)], "h%d_%d" % (g, h))
 
         def second_product(a, h, stores):
             bank = ring_bank()
             for g in range(GROUPS):
-                h_codes, h_plane = h_quant[(g, h)]
+                clipped_codes, clipped_plane = clipped_quant[(g, h)]
                 nc.tensor.matmul_mx(
                     out=bank[:],
                     lhsT=w_codes[:, g, 2 * a * P:2 * (a + 1) * P].bitcast(FP4X4),
                     lhsT_scale=w_plane[:, g, a * P:(a + 1) * P],
-                    rhs=h_codes[:].bitcast(FP8X4), rhs_scale=h_plane[:],
+                    rhs=clipped_codes[:].bitcast(FP8X4), rhs_scale=clipped_plane[:],
                     start=(g == 0), stop=(g == GROUPS - 1))
             width = N // stores
             for part in range(stores):
                 result = work.tile([P, width], F32, name="result", bufs=6)
                 nc.scalar.copy(out=result[:], in_=bank[:, part * width:(part + 1) * width])
-                first = h * N + part * width
-                nc.sync.dma_start(out=out[a * P:(a + 1) * P, first:first + width], in_=result[:])
+                column = h * N + part * width
+                nc.sync.dma_start(out=out[a * P:(a + 1) * P, column:column + width], in_=result[:])
 
-        load_g(0, 0, 2)
-        load_x(0, 0)
-        load_g(0, 2, 2)
-        load_g(1, 0, 2)
-        load_g(1, 2, 2)
-        load_x(1, 0)
-        load_g(2)
-        load_x(2, 0)
-        load_g(3)
-        load_g(4)
-        load_x(3, 0)
-        load_g(5)
+        load_gmap(0, 0, 2)
+        load_base(0, 0)
+        load_gmap(0, 2, 2)
+        load_gmap(1, 0, 2)
+        load_gmap(1, 2, 2)
+        load_base(1, 0)
+        load_gmap(2)
+        load_base(2, 0)
+        load_gmap(3)
+        load_gmap(4)
+        load_base(3, 0)
+        load_gmap(5)
         nc.sync.dma_start(out=bias[:], in_=offset.rearrange("(g p t) -> p g t", p=P, t=PACK))
-        load_x(0, 1)
-        load_g(6)
-        load_g(7)
+        load_base(0, 1)
+        load_gmap(6)
+        load_gmap(7)
         for c in range(1, PASSES):
-            load_x(c, 1)
+            load_base(c, 1)
         for piece in range(2 * PACK, PIECES):
-            load_g(piece)
+            load_gmap(piece)
         load_w()
 
-        warm_up(WARM_FIRST)
-        transpose_g(0, (0,))
-        warm_up(WARM_SECOND)
-        transpose_g(0, (1,))
-        share_interleave_x(0, copy_by_activation)
-        evacuate_g(0, (0,))
-        quantize_x(0, 0)
-        quantize_g_pair(0, 0)
-        evacuate_g(0, (1,))
-        quantize_g_pair(0, 1)
-        transpose_g(1, (0,))
-        evacuate_g(1, (0,))
-        warm_up(WARM_THIRD)
+        transpose_gmap(0)
+        share_interleave_base(0, copy_by_activation)
+        evacuate_gmap(0, (0,))
+        quantize_base(0, 0)
+        quantize_gmap_pair(0, 0)
+        evacuate_gmap(0, (1,))
+        quantize_gmap_pair(0, 1)
+        transpose_gmap(1, (0,))
+        evacuate_gmap(1, (0,))
         group0_pass(0, 0)
-        share_interleave_x(1)
-        quantize_g_pair(1, 0)
-        quantize_x(1, 0)
-        transpose_g(1, (1,))
-        evacuate_g(1, (1,))
-        quantize_g_pair(1, 1)
+        share_interleave_base(1)
+        quantize_gmap_pair(1, 0)
+        quantize_base(1, 0)
+        transpose_gmap(1, (1,))
+        evacuate_gmap(1, (1,))
+        quantize_gmap_pair(1, 1)
         for c in range(2, PASSES):
-            transpose_g(c)
+            transpose_gmap(c)
             group0_pass(c - 1, 0)
-            evacuate_g(c)
+            evacuate_gmap(c)
             if c == PASSES - 1:
-                sort_g(4)
-            share_interleave_x(c)
-            quantize_g(c)
-            quantize_x(c, 0)
+                sort_gmap(4)
+            share_interleave_base(c)
+            quantize_gmap(c)
+            quantize_base(c, 0)
 
         for piece in (4, 5):
-            transpose_g(piece)
-            evacuate_g(piece)
+            transpose_gmap(piece)
+            evacuate_gmap(piece)
         group0_pass(PASSES - 1, 0)
         for t in range(PACK - 1):
             clip(0, t, 0)
-        quantize_g(4)
-        interleave_x(0, 1, 0, N // 2)
-        sort_g(6)
-        interleave_x(0, 1, N // 2, N)
-        sort_g(7)
-        quantize_g(5)
-        quantize_x(0, 1)
+        quantize_gmap(4)
+        interleave_base(0, 1, 0, N // 2)
+        sort_gmap(6)
+        interleave_base(0, 1, N // 2, N)
+        sort_gmap(7)
+        quantize_gmap(5)
+        quantize_base(0, 1)
         first_product(1, 0, 0)
         for piece in (6, 7):
-            transpose_g(piece)
-            evacuate_g(piece)
+            transpose_gmap(piece)
+            evacuate_gmap(piece)
         clip(0, PACK - 1, 0)
         clip(1, 0, 0)
         for c in (2, 3):
-            interleave_x(c, 1, SECOND_HALF_VECTOR_COLS, N, nc.scalar.copy)
-        quantize_g(6)
-        interleave_x(1, 1, 0, N // 2)
-        quantize_g(7)
-        interleave_x(1, 1, N // 2, N)
+            interleave_base(c, 1, SECOND_HALF_VECTOR_COLS, N, nc.scalar.copy)
+        quantize_gmap(6)
+        interleave_base(1, 1, 0, N // 2)
+        quantize_gmap(7)
+        interleave_base(1, 1, N // 2, N)
         for t in range(1, PACK):
             first_product(1, t, 0)
             clip(1, t, 0)
         for c in (2, 3):
-            interleave_x(c, 1, 0, SECOND_HALF_VECTOR_COLS)
-            quantize_x(c - 1, 1)
-        quantize_x(PASSES - 1, 1)
+            interleave_base(c, 1, 0, SECOND_HALF_VECTOR_COLS)
+            quantize_base(c - 1, 1)
+        quantize_base(PASSES - 1, 1)
 
         for c in range(PASSES):
             group0_pass(c, 1)
         for piece in (8, 9):
-            sort_g(piece)
+            sort_gmap(piece)
         for t in range(PACK):
             clip(0, t, 1)
         for piece in (8, 9):
-            transpose_g(piece)
-            evacuate_g(piece)
+            transpose_gmap(piece)
+            evacuate_gmap(piece)
         for piece in (10, 11):
-            sort_g(piece)
-        interleave_h(0, 0)
-        quantize_g(8)
-        quantize_h(0, 0)
-        quantize_g(9)
-        interleave_h(1, 0)
+            sort_gmap(piece)
+        interleave_clipped(0, 0)
+        quantize_gmap(8)
+        quantize_clipped(0, 0)
+        quantize_gmap(9)
+        interleave_clipped(1, 0)
         for t in range(PACK):
             first_product(1, t, 1)
             clip(1, t, 1)
         for piece in (10, 11):
-            transpose_g(piece)
-            evacuate_g(piece)
-        quantize_h(1, 0)
+            transpose_gmap(piece)
+            evacuate_gmap(piece)
+        quantize_clipped(1, 0)
         for piece in (10, 11):
-            quantize_g(piece)
+            quantize_gmap(piece)
 
         for g in range(2):
-            interleave_h(g, 1)
+            interleave_clipped(g, 1)
         for g in range(2):
-            quantize_h(g, 1)
+            quantize_clipped(g, 1)
         for h in range(HALVES):
             for t in range(PACK):
                 first_product(2, t, h)
                 clip(2, t, h)
-            interleave_h(2, h)
-            quantize_h(2, h)
+            interleave_clipped(2, h)
+            quantize_clipped(2, h)
 
         tiles = [(h, a) for h in range(HALVES) for a in range(A // P)]
         for h, a in tiles:

from contextlib import ExitStack

import concourse.mybir as mybir
from concourse.masks import make_identity

A, B, K, T = 512, 1536, 2048, 1024
FLOPS = 2 * B * K * T + 2 * A * B * T

F32 = mybir.dt.float32
BF16 = mybir.dt.bfloat16
I32 = mybir.dt.int32
U32 = mybir.dt.uint32
U8 = mybir.dt.uint8
FP8X4 = mybir.dt.float8_e4m3fn_x4
FP4X4 = mybir.dt.float4_e2m1fn_x4
ACT = mybir.ActivationFunctionType

P = 128
PACK = 4
K_PASS = P * PACK
N = 512
PASSES = K // K_PASS
GROUPS = B // K_PASS
HALVES = T // N
PIECES = GROUPS * PACK
RUN = 4
ALIGN = 256
QUADRANT = 32
SCALE_ROWS = 4
BANKS = 8
HEAD_PIECES = 6

FIRST_HALF_VECTOR_COLS = 384
SECOND_HALF_VECTOR_COLS = 256


def tile_mint_forecast_reconciliation_s13_kernel(tc, gmap, base, offset, w_words, w_scales, out):
    nc = tc.nc
    with ExitStack() as ctx:
        keep = ctx.enter_context(tc.tile_pool(name="keep", bufs=1))
        work = ctx.enter_context(tc.tile_pool(name="work", bufs=2))
        psum = ctx.enter_context(tc.psum_pool(name="psum", bufs=1))
        ctx.enter_context(tc.manual_schedule())

        ident = keep.tile([P, P], F32, name="ident")
        make_identity(nc, ident[:])
        w_codes = keep.tile([P, GROUPS, 2 * A], U8, name="w_codes", align_bytes=ALIGN)
        w_plane = keep.tile([P, GROUPS, A], U8, name="w_plane", align_bytes=ALIGN)
        bias = keep.tile([P, GROUPS, PACK], BF16, name="bias")

        nc.vector.memset(w_plane[:].rearrange("p g a -> p (g a)").bitcast(I32), 0)

        gmap_words, gmap_raw, gmap_sorted, gmap_banks, gmap_grouped, gmap_quant = {}, {}, {}, {}, {}, {}
        base_raw, base_grouped, base_quant = {}, {}, {}
        sums, clipped_raw, clipped_grouped, clipped_quant = {}, {}, {}, {}
        head_banks, ring_banks = [], []

        def bank_tile(number):
            bank = psum.tile([P, N], F32, name="bank%d" % number)
            return bank

        def ring_bank():
            ring_banks.append(bank_tile((BANKS // 2 + len(ring_banks)) % BANKS))
            return ring_banks[-1]

        def head_bank():
            head_banks.append(bank_tile(len(head_banks) % (BANKS // 2)))
            return head_banks[-1]

        def load_gmap(piece, first=0, quarters=PACK):
            g, j = divmod(piece, PACK)
            rows = gmap[g * K_PASS:(g + 1) * K_PASS, :].rearrange("(m t) k -> m t k", t=PACK)
            raw = keep.tile([P, quarters, K_PASS], BF16, name="g_raw%d_%d" % (piece, first), align_bytes=ALIGN)
            if g == 0:
                nc.sync.dma_start(out=raw[:], in_=rows[:, first:first + quarters, j * K_PASS:(j + 1) * K_PASS])
            else:
                nc.sync.dma_start(out=raw[:].rearrange("p c k -> p (c k)"), in_=rows[:, j, :])
            gmap_raw[piece] = raw[:].rearrange("p j k -> p (j k)").bitcast(F32)
            for n in range(quarters):
                gmap_words[(piece, first + n)] = gmap_raw[piece][:, 2 * P * n:2 * P * (n + 1)]

        def load_base(c, h):
            raw = keep.tile([P, PACK, N], BF16, name="x_raw%d_%d" % (c, h), align_bytes=ALIGN)
            rows = base[c * K_PASS:(c + 1) * K_PASS, h * N:(h + 1) * N]
            nc.sync.dma_start(out=raw[:], in_=rows.rearrange("(p j) n -> p j n", j=PACK))
            base_raw[(c, h)] = raw

        def load_w():
            nc.sync.dma_start(out=w_codes[:].bitcast(I32), in_=w_words.rearrange("g p n -> p g n").bitcast(I32))
            for quadrant in range(P // QUADRANT):
                rows = w_scales[:, SCALE_ROWS * quadrant:SCALE_ROWS * (quadrant + 1), :]
                nc.sync.dma_start(
                    out=w_plane[QUADRANT * quadrant:QUADRANT * quadrant + SCALE_ROWS, :, :].bitcast(I32),
                    in_=rows.rearrange("g r a -> r g a").bitcast(I32))

        def sort_gmap(piece):
            ordered = work.tile([P, 2 * K_PASS], F32, name="g_sorted", align_bytes=ALIGN)
            nc.vector.tensor_copy(
                out=ordered[:].rearrange("p (u run i) -> p run u i", u=2, i=RUN),
                in_=gmap_raw[piece].rearrange("p (run i u) -> p run u i", u=2, i=RUN))
            gmap_sorted[piece] = ordered

        def transpose_gmap(piece, pairs=(0, 1)):
            for pair in pairs:
                bank = head_bank() if piece < HEAD_PIECES else ring_bank()
                for n in range(2):
                    quarter = 2 * pair + n
                    for u in range(2):
                        if piece in gmap_sorted:
                            words = gmap_sorted[piece][:, u * K_PASS + quarter * P:u * K_PASS + (quarter + 1) * P]
                        else:
                            words = gmap_words[(piece, quarter)][:, u:2 * P:2]
                        column = (2 * n + u) * P
                        nc.tensor.transpose(bank[:, column:column + P], words, ident[:])
                gmap_banks[(piece, pair)] = bank

        def evacuate_gmap(piece, pairs=(0, 1)):
            if pairs[0] == 0:
                gmap_grouped[piece] = work.tile([P, PACK * N], BF16, name="g_grouped", bufs=3, align_bytes=ALIGN)
            words = gmap_grouped[piece][:].bitcast(F32)
            for pair in pairs:
                nc.scalar.copy(
                    out=words[:, pair * N:(pair + 1) * N].rearrange("p (j r u) -> p j r u", j=2, u=2),
                    in_=gmap_banks[(piece, pair)][:].rearrange("p (j u r) -> p j r u", j=2, u=2))

        def mx_tiles(name):
            codes = keep.tile([P, N], U32, name=name + "_codes", align_bytes=ALIGN)
            plane = keep.tile([P, N], U8, name=name + "_plane", align_bytes=ALIGN)
            return codes, plane

        def quantize(grouped, name):
            codes, plane = mx_tiles(name)
            nc.vector.quantize_mx(out=codes[:].bitcast(FP8X4), scales=plane[:], in_=grouped[:])
            return codes, plane

        def quantize_gmap(piece):
            gmap_quant[piece] = quantize(gmap_grouped[piece], "g%d" % piece)

        def quantize_gmap_pair(piece, pair):
            if pair == 0:
                gmap_quant[piece] = mx_tiles("g%d" % piece)
            codes, plane = gmap_quant[piece]
            cols = slice(pair * 2 * P, (pair + 1) * 2 * P)
            nc.vector.quantize_mx(out=codes[:, cols].bitcast(FP8X4), scales=plane[:, cols],
                                  in_=gmap_grouped[piece][:, PACK * cols.start:PACK * cols.stop])

        def interleave(copy, grouped, raw, lo, hi):
            copy(out=grouped[:, PACK * lo:PACK * hi].rearrange("p (run i t) -> p run t i", i=RUN, t=PACK),
                 in_=raw[:, :, lo:hi].rearrange("p t (run i) -> p run t i", i=RUN))

        def interleave_base(c, h, lo=0, hi=N, copy=nc.vector.tensor_copy):
            if (c, h) not in base_grouped:
                base_grouped[(c, h)] = work.tile([P, PACK * N], BF16, name="x_grouped", bufs=3, align_bytes=ALIGN)
            interleave(copy, base_grouped[(c, h)], base_raw[(c, h)], lo, hi)

        def share_interleave_base(c, scalar_copy=nc.scalar.copy):
            interleave_base(c, 0, 0, FIRST_HALF_VECTOR_COLS)
            interleave_base(c, 0, FIRST_HALF_VECTOR_COLS, N, scalar_copy)

        def copy_by_activation(out, in_):
            nc.scalar.activation(out=out, in_=in_, func=ACT.Copy)

        def quantize_base(c, h):
            base_quant[(c, h)] = quantize(base_grouped[(c, h)], "x%d_%d" % (c, h))

        def first_pass(g, t, h, c):
            if c == 0:
                sums[(g, t, h)] = ring_bank()
            piece, quarter = (c, t) if g == 0 else (PACK * g + t, c)
            gmap_codes, gmap_plane = gmap_quant[piece]
            base_codes, base_plane = base_quant[(c, h)]
            cols = slice(quarter * P, (quarter + 1) * P)
            nc.tensor.matmul_mx(
                out=sums[(g, t, h)][:],
                lhsT=gmap_codes[:, cols].bitcast(FP8X4), lhsT_scale=gmap_plane[:, cols],
                rhs=base_codes[:].bitcast(FP8X4), rhs_scale=base_plane[:],
                start=(c == 0), stop=(c == PASSES - 1))

        def first_product(g, t, h):
            for c in range(PASSES):
                first_pass(g, t, h, c)

        def group0_pass(c, h):
            for t in range(PACK):
                first_pass(0, t, h, c)

        def clip(g, t, h):
            if t == 0:
                clipped_raw[(g, h)] = work.tile([P, PACK, N], BF16, name="h_raw", bufs=4, align_bytes=ALIGN)
            nc.scalar.activation(out=clipped_raw[(g, h)][:, t, :], in_=sums[(g, t, h)][:], func=ACT.Relu,
                                 bias=bias[:, g, t:t + 1])

        def interleave_clipped(g, h):
            grouped = work.tile([P, PACK * N], BF16, name="h_grouped", align_bytes=ALIGN)
            interleave(nc.vector.tensor_copy, grouped, clipped_raw[(g, h)], 0, N)
            clipped_grouped[(g, h)] = grouped

        def quantize_clipped(g, h):
            clipped_quant[(g, h)] = quantize(clipped_grouped[(g, h)], "h%d_%d" % (g, h))

        def second_product(a, h, stores):
            bank = ring_bank()
            for g in range(GROUPS):
                clipped_codes, clipped_plane = clipped_quant[(g, h)]
                nc.tensor.matmul_mx(
                    out=bank[:],
                    lhsT=w_codes[:, g, 2 * a * P:2 * (a + 1) * P].bitcast(FP4X4),
                    lhsT_scale=w_plane[:, g, a * P:(a + 1) * P],
                    rhs=clipped_codes[:].bitcast(FP8X4), rhs_scale=clipped_plane[:],
                    start=(g == 0), stop=(g == GROUPS - 1))
            width = N // stores
            for part in range(stores):
                result = work.tile([P, width], F32, name="result", bufs=6)
                nc.scalar.copy(out=result[:], in_=bank[:, part * width:(part + 1) * width])
                column = h * N + part * width
                nc.sync.dma_start(out=out[a * P:(a + 1) * P, column:column + width], in_=result[:])

        load_gmap(0, 0, 2)
        load_base(0, 0)
        load_gmap(0, 2, 2)
        load_gmap(1, 0, 2)
        load_gmap(1, 2, 2)
        load_base(1, 0)
        load_gmap(2)
        load_base(2, 0)
        load_gmap(3)
        load_gmap(4)
        load_base(3, 0)
        load_gmap(5)
        nc.sync.dma_start(out=bias[:], in_=offset.rearrange("(g p t) -> p g t", p=P, t=PACK))
        load_base(0, 1)
        load_gmap(6)
        load_gmap(7)
        for c in range(1, PASSES):
            load_base(c, 1)
        for piece in range(2 * PACK, PIECES):
            load_gmap(piece)
        load_w()

        transpose_gmap(0)
        share_interleave_base(0, copy_by_activation)
        evacuate_gmap(0, (0,))
        quantize_base(0, 0)
        quantize_gmap_pair(0, 0)
        evacuate_gmap(0, (1,))
        quantize_gmap_pair(0, 1)
        transpose_gmap(1, (0,))
        evacuate_gmap(1, (0,))
        group0_pass(0, 0)
        share_interleave_base(1)
        quantize_gmap_pair(1, 0)
        quantize_base(1, 0)
        transpose_gmap(1, (1,))
        evacuate_gmap(1, (1,))
        quantize_gmap_pair(1, 1)
        for c in range(2, PASSES):
            transpose_gmap(c)
            group0_pass(c - 1, 0)
            evacuate_gmap(c)
            if c == PASSES - 1:
                sort_gmap(4)
            share_interleave_base(c)
            quantize_gmap(c)
            quantize_base(c, 0)

        for piece in (4, 5):
            transpose_gmap(piece)
            evacuate_gmap(piece)
        group0_pass(PASSES - 1, 0)
        for t in range(PACK - 1):
            clip(0, t, 0)
        quantize_gmap(4)
        interleave_base(0, 1, 0, N // 2)
        sort_gmap(6)
        interleave_base(0, 1, N // 2, N)
        sort_gmap(7)
        quantize_gmap(5)
        quantize_base(0, 1)
        first_product(1, 0, 0)
        for piece in (6, 7):
            transpose_gmap(piece)
            evacuate_gmap(piece)
        clip(0, PACK - 1, 0)
        clip(1, 0, 0)
        for c in (2, 3):
            interleave_base(c, 1, SECOND_HALF_VECTOR_COLS, N, nc.scalar.copy)
        quantize_gmap(6)
        interleave_base(1, 1, 0, N // 2)
        quantize_gmap(7)
        interleave_base(1, 1, N // 2, N)
        for t in range(1, PACK):
            first_product(1, t, 0)
            clip(1, t, 0)
        for c in (2, 3):
            interleave_base(c, 1, 0, SECOND_HALF_VECTOR_COLS)
            quantize_base(c - 1, 1)
        quantize_base(PASSES - 1, 1)

        for c in range(PASSES):
            group0_pass(c, 1)
        for piece in (8, 9):
            sort_gmap(piece)
        for t in range(PACK):
            clip(0, t, 1)
        for piece in (8, 9):
            transpose_gmap(piece)
            evacuate_gmap(piece)
        for piece in (10, 11):
            sort_gmap(piece)
        interleave_clipped(0, 0)
        quantize_gmap(8)
        quantize_clipped(0, 0)
        quantize_gmap(9)
        interleave_clipped(1, 0)
        for t in range(PACK):
            first_product(1, t, 1)
            clip(1, t, 1)
        for piece in (10, 11):
            transpose_gmap(piece)
            evacuate_gmap(piece)
        quantize_clipped(1, 0)
        for piece in (10, 11):
            quantize_gmap(piece)

        for g in range(2):
            interleave_clipped(g, 1)
        for g in range(2):
            quantize_clipped(g, 1)
        for h in range(HALVES):
            for t in range(PACK):
                first_product(2, t, h)
                clip(2, t, h)
            interleave_clipped(2, h)
            quantize_clipped(2, h)

        tiles = [(h, a) for h in range(HALVES) for a in range(A // P)]
        for h, a in tiles:
            second_product(a, h, 2 if (h, a) == tiles[-1] else 1)
